import numpy as np
import ml_dtypes


def mxq(x, axis, fmt="e4m3"):
    dtype, down = {"e4m3": (ml_dtypes.float8_e4m3fn, 7), "e5m2": (ml_dtypes.float8_e5m2, 14)}[fmt]
    v = np.moveaxis(np.asarray(x, np.float32).astype(ml_dtypes.bfloat16).astype(np.float64), axis, -1)
    blocks = v.reshape(v.shape[:-1] + (-1, 32))
    amax = np.abs(blocks).max(-1, keepdims=True)
    byte = np.maximum(np.where(amax > 0, np.frexp(amax)[1] - 1 + 127, 0) - down, 1)
    scale = np.exp2(byte - 127.0)
    codes = (blocks / scale).astype(np.float32).astype(dtype).astype(np.float64)
    return np.moveaxis((codes * scale).reshape(v.shape), -1, axis)


WIDE = False


def mx_kscale(k):
    if not WIDE:
        return np.ones(k)
    levels = np.array([10, -10, 5, -5, 0])
    if k % 512:
        return np.exp2(np.random.permutation(np.resize(levels, k // 32))).repeat(32)
    a = np.empty((k // 512, 16))
    for p in range(k // 512):
        a[p, :8] = np.random.permutation(np.resize(levels, 8))
        for g in range(8):
            far = levels[np.abs(levels - a[p, g]) >= 10]
            a[p, g + 8] = far[np.random.randint(len(far))]
    return np.exp2(a.ravel()).repeat(32)


BF16 = ml_dtypes.bfloat16


def bf(x):
    return np.asarray(x, np.float32).astype(BF16)


def f64(x):
    return np.asarray(x).astype(np.float64)


E2M1 = np.array([0.0, 0.5, 1.0, 1.5, 2.0, 3.0, 4.0, 6.0, -0.0, -0.5, -1.0, -1.5, -2.0, -3.0, -4.0, -6.0])


def pack_weight(w, fmt):
    k, n = w.shape
    w = f64(bf(w)).reshape(k // 32, 32, n)
    amax = np.abs(w).max(1)
    if fmt == "e4m3":
        byte = np.frexp(amax)[1] - 1 + 127 - 7
    else:
        mant, ex = np.frexp(amax / 6.0)
        byte = np.where(mant > 0.5, ex, ex - 1) + 127
    byte = np.clip(np.where(amax > 0, byte, 1), 1, 254)
    scaled = (w * np.exp2(127.0 - byte)[:, None, :]).reshape(k, n).astype(np.float32)
    by_word = np.ascontiguousarray(scaled.reshape(k // 512, 128, 4, n).transpose(0, 1, 3, 2))
    if fmt == "e4m3":
        words = by_word.astype(ml_dtypes.float8_e4m3fn).view(np.uint8)
    else:
        c = by_word.astype(ml_dtypes.float4_e2m1fn).view(np.uint8) & 0xF
        words = c[..., 0::2] | (c[..., 1::2] << 4)
    return np.ascontiguousarray(words), np.ascontiguousarray(byte.astype(np.uint8).reshape(k // 512, 16, n))


def unpack_weight(words, scales, fmt):
    g, p, n, _ = words.shape
    if fmt == "e4m3":
        vals = np.ascontiguousarray(words).view(ml_dtypes.float8_e4m3fn).astype(np.float64)
    else:
        nib = np.empty((g, p, n, 4), np.uint8)
        nib[..., 0::2] = words & 0xF
        nib[..., 1::2] = words >> 4
        vals = E2M1[nib]
    vals = vals * np.repeat(np.exp2(scales.astype(np.float64) - 127.0), 8, axis=1)[..., None]
    return vals.transpose(0, 1, 3, 2).reshape(g * 512, n)
def pack4(w):
    words, scales = pack_weight(w, "e2m1")
    return words.reshape(words.shape[0], 128, -1), scales


def unpack4(words, scales):
    return unpack_weight(words.reshape(words.shape[0], 128, -1, 2), scales, "e2m1")


N, D, FA, FB = 1024, 1024, 1024, 1024


def _weighted_center(h, t, n):
    mean = np.sum(t[:, None] * h, axis=0)[None, :] / n
    return h - mean


def _weighted_square_sum(c, t):
    return np.sum(t[:, None] * np.square(c), axis=0)


def draw0():
    s, u = mx_kscale(D), mx_kscale(N)
    r = 0.4 + 1.2 * np.random.random_sample(N)
    x = np.random.standard_normal((N, D)) * r[:, None]
    wa = np.random.standard_normal((D, FA)) / np.sqrt(D) * (0.5 + np.random.random_sample(FA))
    wb = np.random.standard_normal((D, FB)) / np.sqrt(D) * (0.5 + np.random.random_sample(FB))
    p = r * (0.8 + 0.4 * np.random.random_sample(N))
    q = 0.5 + np.random.random_sample(N)
    wa_words, wa_scales = pack4(wa / s[:, None])
    wb_words, wb_scales = pack4(wb / s[:, None])
    return {"x": bf(x * s), "wa_words": wa_words, "wa_scales": wa_scales, "wb_words": wb_words, "wb_scales": wb_scales, "p": bf(p * u), "q": bf(q / u)}


def core(x, wa_words, wa_scales, wb_words, wb_scales, p, q):
    p, q = f64(p), f64(q)
    xq = mxq(f64(x), 1, "e4m3")
    ha = np.maximum(xq @ unpack4(wa_words, wa_scales), 0.0)
    hb = np.maximum(xq @ unpack4(wb_words, wb_scales), 0.0)

    t = p * q
    n = np.sum(t)

    ca = _weighted_center(ha, t, n)
    cb = _weighted_center(hb, t, n)

    va = _weighted_square_sum(ca, t)
    vb = _weighted_square_sum(cb, t)

    k = mxq((p[:, None] * ca).T, 1, "e4m3") @ mxq(q[:, None] * cb, 0, "e4m3")

    return 32.0 * k / (np.sqrt(va)[:, None] * np.sqrt(vb)[None, :])


def e4m3fn_bytes(y):
    return np.clip(np.asarray(y, np.float64), -448.0, 448.0).astype(np.float32).astype(ml_dtypes.float8_e4m3fn).view(np.uint8)


def e4m3fn_values(b):
    return np.asarray(b, np.uint8).view(ml_dtypes.float8_e4m3fn).astype(np.float64)


def setup_inputs():
    d = draw0()
    x0 = np.asarray(d['x']).astype(np.float64)
    s = (np.max(np.abs(x0), axis=(0,), keepdims=True) / 448.0).astype(np.float32)
    out = {}
    for k, v in d.items():
        if k == 'x':
            out['x_bytes'] = e4m3fn_bytes(x0 / s.astype(np.float64))
            out['x_scale'] = s
        else:
            out[k] = v
    return out


def reference(x_bytes, x_scale, wa_words, wa_scales, wb_words, wb_scales, p, q):
    return core(e4m3fn_values(x_bytes) * x_scale.astype(np.float64), wa_words, wa_scales, wb_words, wb_scales, p, q)

@@ -1,0 +1,400 @@
+from contextlib import ExitStack
+from functools import partial
+
+import concourse.mybir as mybir
+from concourse.masks import make_identity
+
+F32 = mybir.dt.float32
+BF16 = mybir.dt.bfloat16
+I32 = mybir.dt.int32
+U32 = mybir.dt.uint32
+U8 = mybir.dt.uint8
+FP8 = mybir.dt.float8_e4m3fn
+FP8X4 = mybir.dt.float8_e4m3fn_x4
+FP4X4 = mybir.dt.float4_e2m1fn_x4
+ALU = mybir.AluOpType
+ACT = mybir.ActivationFunctionType
+AX = mybir.AxisListType
+
+P = 128
+N_TOK = 1024
+D_IN = 1024
+N_FEAT = 1024
+CH = 512
+TILES = 8
+FB = CH // P
+FLOPS = 3 * 2 * 1024 * 1024 * 1024
+
+ON_POOL = [(0, 1), (1, 1), (2, 1), (3, 0)]
+CAST_V = [(0, 0), (0, 1), (0, 2), (0, 3)]
+IL_S = []
+OUT_BANKS = [2, 3, 4, 5, 6, 1, 2, 3, 4, 5, 6, 1, 0, 2, 3, 7]
+CHUNKS = [(1, 0), (0, 0), (1, 1), (0, 1)]
+
+
+def tile_zipitweightedfeaturecorrelation_w4_kernel(
+    tc, x_bytes, x_scale, wa_words, wa_scales, wb_words, wb_scales, p, q, out
+):
+    nc = tc.nc
+    with ExitStack() as ctx:
+        sb = ctx.enter_context(tc.tile_pool(name="sb", bufs=1))
+        ps = ctx.enter_context(tc.psum_pool(name="ps", bufs=1))
+        ctx.enter_context(tc.manual_schedule())
+
+        def sbt(name, shape, dtype):
+            return sb.tile(shape, dtype, name=name, align_bytes=64)
+
+        banks = [ps.tile([P, CH], F32, name="bank%d" % i) for i in range(8)]
+        x_banks = [banks[0], banks[1], banks[7]]
+        mean_banks = [banks[1], banks[0]]
+        h_banks = banks[2:6]
+        macc = banks[6]
+        vacc = banks[7]
+
+        ident = sbt("ident", [P, P], F32)
+        p_sb = sbt("p_sb", [P, 2, 4], BF16)
+        q_sb = sbt("q_sb", [P, 2, 4], BF16)
+        xs_sb = sbt("xs_sb", [P, 2, 4], F32)
+        xraw = [sbt("xraw0", [P, 1, D_IN], U8), sbt("xraw1", [P, 1, D_IN], U8),
+                sbt("xraw2", [P, 2, D_IN], U8), sbt("xraw3", [P, 4, D_IN], U8)]
+        xsrc = [(0, 0), (1, 0), (2, 0), (2, 1), (3, 0), (3, 1), (3, 2), (3, 3)]
+        xwide = [sbt("xwide%d" % i, [P, D_IN], BF16) for i in range(TILES)]
+        xil = [sbt("xil%d" % i, [P, D_IN], BF16) for i in range(4)]
+        xcodes = [sbt("xcodes%d" % i, [P, 2 * P], U32) for i in range(TILES)]
+        xscales = [sbt("xscales%d" % i, [P, 2 * P], U8) for i in range(TILES)]
+        wwords = [sbt("wwords%d" % c, [P, 2, 2 * CH], U8) for c in range(4)]
+        wscales = [sbt("wscales%d" % m, [P, 2, N_FEAT], U8) for m in range(2)]
+        th4 = [[sbt("th%d_%d" % (c, g), [P, 4, CH], F32) for g in range(2)] for c in range(4)]
+        th = [[th4[c][j // 4][:, j % 4, :] for j in range(TILES)] for c in range(4)]
+        sq = [sbt("sq%d" % i, [P, CH], F32) for i in range(2 * TILES)]
+        planes = [sbt("planes%d" % i, [P, 4, CH], BF16) for i in range(2)]
+        inter = [sbt("inter%d" % i, [P, 4 * CH], BF16) for i in range(4)]
+        codes = [[sbt("codes%d_%d" % (c, g), [P, CH], U32) for g in range(2)] for c in range(4)]
+        cscales = [[sbt("cscales%d_%d" % (c, g), [P, CH], U8) for g in range(2)] for c in range(4)]
+        t_sb = sbt("t_sb", [P, TILES], F32)
+        root_t = sbt("root_t", [P, TILES], F32)
+        rroot_t = sbt("rroot_t", [P, TILES], F32)
+        inv_other = [sbt("inv_q", [P, TILES], F32), sbt("inv_p", [P, TILES], F32)]
+        t_row = sbt("t_row", [P, 1], F32)
+        n_sb = sbt("n_sb", [P, 1], F32)
+        inv_n = sbt("inv_n", [P, 1], F32)
+        neg_tn = sbt("neg_tn", [P, TILES], F32)
+        msum = [sbt("msum%d" % c, [P, FB], F32) for c in range(4)]
+        vsum = [sbt("vsum%d" % c, [P, FB], F32) for c in range(4)]
+        vroot = [sbt("vroot%d" % c, [P, FB], F32) for c in range(4)]
+        rinv = [sbt("rinv%d" % c, [P, FB], F32) for c in range(4)]
+        rb_rows = [sbt("rb_rows%d" % h, [P, CH], F32) for h in range(2)]
+        ostage = [sbt("ostage%d" % i, [P, CH], F32) for i in range(8)]
+
+        words_in = [wa_words, wb_words]
+        scales_in = [wa_scales, wb_scales]
+
+        nc.scalar.dma_start(out=p_sb[:], in_=p.rearrange("(g m t) -> m g t", g=2, t=4))
+        nc.scalar.dma_start(out=q_sb[:], in_=q.rearrange("(g m t) -> m g t", g=2, t=4))
+        nc.scalar.dma_start(out=xs_sb[:], in_=x_scale.rearrange("o (g m t) -> m (o g) t", g=2, t=4))
+        for m in (1, 0):
+            nc.vector.memset(wscales[m][:].rearrange("p g n -> p (g n)").bitcast(I32), 0)
+        make_identity(nc, ident[:])
+
+        x_rows = x_bytes.rearrange("(g m t) k -> g m t k", g=2, t=4)
+
+        def load_words(c):
+            m, h = CHUNKS[c]
+            nc.sync.dma_start(
+                out=wwords[c][:].bitcast(I32),
+                in_=words_in[m].rearrange("g p n -> p g n")[:, :, 2 * CH * h : 2 * CH * (h + 1)].bitcast(I32),
+            )
+
+        def load_scales(m):
+            for quad in range(4):
+                nc.sync.dma_start(
+                    out=wscales[m][32 * quad : 32 * quad + 4, :, :].bitcast(I32),
+                    in_=scales_in[m].rearrange("g r n -> r g n")[4 * quad : 4 * quad + 4, :, :].bitcast(I32),
+                )
+
+        nc.sync.dma_start(out=xraw[0][:], in_=x_rows[0][:, 0:1, :])
+        nc.sync.dma_start(out=xraw[1][:], in_=x_rows[0][:, 1:2, :])
+        nc.sync.dma_start(out=xraw[2][:], in_=x_rows[0][:, 2:4, :])
+        load_scales(1)
+        load_words(0)
+        nc.sync.dma_start(out=xraw[3][:], in_=x_rows[1])
+        load_scales(0)
+        for c in range(1, 4):
+            load_words(c)
+
+        p_flat = p_sb[:].rearrange("p g t -> p (g t)")
+        q_flat = q_sb[:].rearrange("p g t -> p (g t)")
+        nc.vector.tensor_tensor(out=t_sb[:], in0=p_flat, in1=q_flat, op=ALU.mult)
+        nc.scalar.activation(out=root_t[:], in_=t_sb[:], func=ACT.Sqrt)
+        nc.vector.reciprocal(out=inv_other[0][:], in_=q_flat)
+        nc.vector.reciprocal(out=inv_other[1][:], in_=p_flat)
+        nc.vector.tensor_reduce(out=t_row[:], in_=t_sb[:], axis=AX.X, op=ALU.add)
+        nc.vector.reciprocal(out=rroot_t[:], in_=root_t[:])
+
+        def spread(bank, col0, column):
+            nc.tensor.transpose(bank[:, col0 : col0 + P], column.to_broadcast([P, P]), ident[:])
+
+        def weights_n():
+            nc.vector.tensor_reduce(out=n_sb[:], in_=macc[:, 0:P], axis=AX.X, op=ALU.add)
+            nc.vector.reciprocal(out=inv_n[:], in_=n_sb[:])
+            nc.vector.tensor_scalar(
+                out=neg_tn[:], in0=t_sb[:], scalar1=inv_n[:, 0:1], scalar2=-1.0, op0=ALU.mult, op1=ALU.mult
+            )
+
+        def widen_x(j):
+            i, r = xsrc[j]
+            nc.scalar.copy(out=xwide[j][:], in_=xraw[i][:, r, :].bitcast(FP8))
+
+        def turn_x(j):
+            words = xwide[j][:].bitcast(F32)
+            for g in range(2):
+                for u in range(2):
+                    col = (2 * g + u) * P
+                    nc.tensor.transpose(
+                        x_banks[j % 3][:, col : col + P], words[:, 256 * g + u : 256 * (g + 1) : 2], ident[:]
+                    )
+
+        def scale_x(j, g):
+            src = x_banks[j % 3][:].bitcast(BF16).rearrange("p (g u r e) -> p g r u e", g=2, u=2, e=2)
+            dst = xil[j % 4][:].rearrange("p (g r u e) -> p g r u e", g=2, u=2, e=2)
+            sc = xs_sb[:, g, :].rearrange("p (u e) -> p u e", u=2).unsqueeze(1).to_broadcast([P, P, 2, 2])
+            nc.vector.tensor_tensor(out=dst[:, g, :, :, :], in0=src[:, g, :, :, :], in1=sc, op=ALU.mult)
+
+        def quant_x(j):
+            nc.vector.quantize_mx(out=xcodes[j][:].bitcast(FP8X4), scales=xscales[j][:], in_=xil[j % 4][:])
+
+        def first_product(c, j):
+            m, h = CHUNKS[c]
+            for g in range(2):
+                nc.tensor.matmul_mx(
+                    out=h_banks[j % 4][:],
+                    lhsT=xcodes[j][:, g * P : (g + 1) * P].bitcast(FP8X4),
+                    lhsT_scale=xscales[j][:, g * P : (g + 1) * P],
+                    rhs=wwords[c][:, g, :].bitcast(FP4X4),
+                    rhs_scale=wscales[m][:, g, h * CH : (h + 1) * CH],
+                    start=(g == 0),
+                    stop=(g == 1),
+                )
+
+        def relu_out(c, j):
+            nc.scalar.activation(out=th[c][j], in_=h_banks[j % 4][:], func=ACT.Relu, scale=t_sb[:, j : j + 1])
+
+        def add_turned(acc, src, j):
+            for f in range(FB):
+                nc.tensor.matmul(
+                    out=acc[:, f * P : (f + 1) * P],
+                    lhsT=src[:, f * P : (f + 1) * P],
+                    rhs=ident[:],
+                    is_transpose=True,
+                    start=(j == 0 and f == 0),
+                    stop=(j == TILES - 1 and f == FB - 1),
+                )
+
+        def sum_tokens(dst, acc):
+            nc.vector.tensor_reduce(
+                out=dst[:], in_=acc[:].rearrange("p (f m) -> p f m", f=FB), axis=AX.X, op=ALU.add
+            )
+
+        def centre(c, j):
+            nc.vector.scalar_tensor_tensor(
+                out=th[c][j], in0=mean_banks[c % 2][:], scalar=neg_tn[:, j : j + 1], in1=th[c][j],
+                op0=ALU.mult, op1=ALU.add,
+            )
+
+        def square(c, j):
+            nc.scalar.activation(
+                out=sq[(c % 2) * TILES + j][:], in_=th[c][j], func=ACT.Square, scale=rroot_t[:, j : j + 1]
+            )
+
+        def cast(c, j, on_vector):
+            inv = inv_other[CHUNKS[c][0]][:, j : j + 1]
+            dst = planes[j // 4][:, j % 4, :]
+            if on_vector:
+                nc.vector.tensor_scalar(out=dst, in0=th[c][j], scalar1=inv, scalar2=None, op0=ALU.mult)
+            else:
+                nc.scalar.activation(out=dst, in_=th[c][j], func=ACT.Copy, scale=inv)
+
+        def interleave(c, g, h):
+            half = CH // 2
+            dst = inter[(c % 2) * 2 + g][:, 4 * half * h : 4 * half * (h + 1)].rearrange("p (c i t) -> p c t i", i=4, t=4)
+            src = planes[g][:, :, half * h : half * (h + 1)].rearrange("p t (c i) -> p c t i", i=4)
+            if (c, g, h) in IL_S:
+                nc.scalar.copy(out=dst, in_=src)
+            else:
+                nc.vector.tensor_copy(out=dst, in_=src)
+
+        def scale_interleave(c, g):
+            inv = inv_other[CHUNKS[c][0]][:, 4 * g : 4 * g + 4].unsqueeze(1).to_broadcast([P, CH, 4])
+            nc.gpsimd.tensor_tensor(
+                out=inter[(c % 2) * 2 + g][:].rearrange("p (f t) -> p f t", t=4),
+                in0=th4[c][g][:].rearrange("p t f -> p f t"),
+                in1=inv,
+                op=ALU.mult,
+            )
+
+        def quant(c, g):
+            nc.vector.quantize_mx(out=codes[c][g][:].bitcast(FP8X4), scales=cscales[c][g][:], in_=inter[(c % 2) * 2 + g][:])
+
+        def norm_root(c):
+            scale = 1.0 / 1024.0 if CHUNKS[c][0] == 0 else 1.0
+            nc.scalar.activation(out=vroot[c][:], in_=vsum[c][:], func=ACT.Sqrt, scale=scale)
+
+        def second_product(bank, ca, f, cb):
+            for g in range(2):
+                nc.tensor.matmul_mx(
+                    out=bank[:],
+                    lhsT=codes[ca][g][:, f * P : (f + 1) * P].bitcast(FP8X4),
+                    lhsT_scale=cscales[ca][g][:, f * P : (f + 1) * P],
+                    rhs=codes[cb][g][:].bitcast(FP8X4),
+                    rhs_scale=cscales[cb][g][:],
+                    start=(g == 0),
+                    stop=(g == 1),
+                )
+
+        def finish(bank, i, ca, f, cb):
+            ha, hb = CHUNKS[ca][1], CHUNKS[cb][1]
+            st = ostage[i % 8]
+            nc.vector.scalar_tensor_tensor(
+                out=st[:], in0=bank[:], scalar=rinv[ca][:, f : f + 1], in1=rb_rows[hb][:],
+                op0=ALU.mult, op1=ALU.mult,
+            )
+            row = ha * CH + f * P
+            nc.sync.dma_start(out=out[row : row + P, hb * CH : (hb + 1) * CH], in_=st[:])
+
+        def mean_sum(c, j):
+            add_turned(macc, th[c][j], j)
+
+        def var_sum(c, j):
+            add_turned(vacc, sq[(c % 2) * TILES + j][:], j)
+
+        def spread_mean(c):
+            for f in range(FB):
+                spread(mean_banks[c % 2], f * P, msum[c][:, f : f + 1])
+
+        def spread_rb(c):
+            for f in range(FB):
+                spread(vacc, f * P, rinv[c][:, f : f + 1])
+
+        def copy_rb(c):
+            nc.scalar.copy(out=rb_rows[CHUNKS[c][1]][:], in_=vacc[:])
+
+        def recip(c):
+            nc.vector.reciprocal(out=rinv[c][:], in_=vroot[c][:])
+
+        steps = {}
+        last_write = {}
+        readers = {}
+
+        def step(key, call, reads, writes):
+            after = set()
+            for r in reads + writes:
+                if r in last_write:
+                    after.add(last_write[r])
+            for w in writes:
+                after = after | set(readers.get(w, []))
+                readers[w] = []
+                last_write[w] = key
+            for r in reads:
+                readers.setdefault(r, []).append(key)
+            steps[key] = (call, after - {key})
+
+        x_bank_no = [0, 1, 7]
+        step(("spread_t",), lambda: spread(macc, 0, t_row[:, 0:1]), [], [("bank", 6)])
+        step(("n",), weights_n, [("bank", 6)], ["n"])
+        for j in range(TILES):
+            xb = ("bank", x_bank_no[j % 3])
+            step(("widen", j), partial(widen_x, j), [], [("xwide", j)])
+            step(("turn", j), partial(turn_x, j), [("xwide", j)], [xb])
+            for g in range(2):
+                step(("scale", j, g), partial(scale_x, j, g), [xb], [("xil", j % 4, g)])
+            step(("xq", j), partial(quant_x, j), [("xil", j % 4, 0), ("xil", j % 4, 1)], [("xc", j)])
+        out_tiles = {1: [(1, f, 0) for f in range(FB)], 2: [(1, f, 2) for f in range(FB)],
+                     3: [(3, f, cb) for f in range(FB) for cb in (0, 2)]}
+        n_out = 0
+        for c in range(4):
+            for j in range(TILES):
+                hb = ("bank", 2 + j % 4)
+                step(("mx", c, j), partial(first_product, c, j), [("xc", j)], [hb])
+                step(("relu", c, j), partial(relu_out, c, j), [hb], [("th", c, j)])
+                step(("msum", c, j), partial(mean_sum, c, j), [("th", c, j)], [("bank", 6)])
+            step(("mred", c), partial(sum_tokens, msum[c], macc), [("bank", 6)], [("m", c)])
+            step(("mspread", c), partial(spread_mean, c), [("m", c)], [("bank", 1 - c % 2)])
+            for j in range(TILES):
+                step(("centre", c, j), partial(centre, c, j), [("bank", 1 - c % 2), "n"], [("th", c, j)])
+                step(("sq", c, j), partial(square, c, j), [("th", c, j)], [("sq", c % 2, j)])
+                step(("vsum", c, j), partial(var_sum, c, j), [("sq", c % 2, j)], [("bank", 7)])
+            for g in range(2):
+                group = [("th", c, j) for j in range(4 * g, 4 * g + 4)]
+                if (c, g) in ON_POOL:
+                    step(("pool", c, g), partial(scale_interleave, c, g), group, [("inter", c % 2, g, h) for h in range(2)])
+                else:
+                    for j in range(4 * g, 4 * g + 4):
+                        step(("cast", c, j), partial(cast, c, j, (c, j) in CAST_V), [("th", c, j)], [("plane", j)])
+                    for h in range(2):
+                        step(("il", c, g, h), partial(interleave, c, g, h),
+                             [("plane", j) for j in range(4 * g, 4 * g + 4)], [("inter", c % 2, g, h)])
+                step(("q", c, g), partial(quant, c, g), [("inter", c % 2, g, h) for h in range(2)], [("codes", c, g)])
+            step(("vred", c), partial(sum_tokens, vsum[c], vacc), [("bank", 7)], [("v", c)])
+            step(("root", c), partial(norm_root, c), [("v", c)], [("root", c)])
+            step(("recip", c), partial(recip, c), [("root", c)], [("rinv", c)])
+            if CHUNKS[c][0] == 1:
+                step(("rbspread", c), partial(spread_rb, c), [("rinv", c)], [("bank", 7)])
+                step(("rbcopy", c), partial(copy_rb, c), [("bank", 7)], [("rb", c)])
+        for c in range(1, 4):
+            for ca, f, cb in out_tiles[c]:
+                ob = OUT_BANKS[n_out]
+                needs = [("codes", k, g) for k in (ca, cb) for g in range(2)]
+                step(("mx2", n_out), partial(second_product, banks[ob], ca, f, cb), needs, [("bank", ob)])
+                step(("fin", n_out), partial(finish, banks[ob], n_out, ca, f, cb),
+                     [("bank", ob), ("rinv", ca), ("rb", cb)], [("ostage", n_out % 8)])
+                n_out = n_out + 1
+
+        def run(name, c, lo, hi):
+            return [(name, c, j) for j in range(lo, hi)]
+
+        def each(name, lo, hi):
+            return [(name, k) for k in range(lo, hi)]
+
+        def il(c, g):
+            return [("il", c, g, 0), ("il", c, g, 1)]
+
+        pe = [("spread_t",)] + each("turn", 0, 3) + run("mx", 0, 0, 1) + each("turn", 3, 5) + run("mx", 0, 1, 3)
+        pe = pe + each("turn", 5, 7) + run("mx", 0, 3, 4) + each("turn", 7, 8) + run("msum", 0, 0, 3) + run("mx", 0, 4, 7)
+        pe = pe + run("msum", 0, 3, 6) + run("mx", 0, 7, 8) + run("mx", 1, 0, 1) + run("msum", 0, 6, 8) + run("mx", 1, 1, 4)
+        pe = pe + [("mspread", 0)] + run("msum", 1, 0, 4) + run("mx", 1, 4, 8) + run("msum", 1, 4, 8)
+        pe = pe + run("mx", 2, 0, 4) + [("mspread", 1)] + run("msum", 2, 0, 4) + run("mx", 2, 4, 8) + run("vsum", 0, 0, 2) + run("msum", 2, 4, 8)
+        pe = pe + run("mx", 3, 0, 4) + [("mspread", 2)] + run("vsum", 0, 2, 8) + run("msum", 3, 0, 4) + run("mx", 3, 4, 8) + [("rbspread", 0)] + run("msum", 3, 4, 8)
+        pe = pe + run("vsum", 1, 0, 4) + [("mspread", 3)] + run("vsum", 1, 4, 8) + each("mx2", 0, 4) + run("vsum", 2, 0, 8)
+        pe = pe + [("rbspread", 2)] + each("mx2", 4, 8) + run("vsum", 3, 0, 8) + each("mx2", 8, 16)
+
+        act = each("widen", 0, 7) + run("relu", 0, 0, 1) + each("widen", 7, 8) + run("relu", 0, 1, 8) + run("relu", 1, 0, 4)
+        act = act + run("sq", 0, 0, 2) + run("relu", 1, 4, 8) + run("sq", 0, 2, 4) + run("relu", 2, 0, 4) + run("sq", 0, 4, 7)
+        act = act + run("relu", 2, 4, 8) + run("cast", 1, 0, 4) + run("sq", 0, 7, 8) + run("relu", 3, 0, 4) + run("sq", 1, 0, 3) + [("root", 0)]
+        act = act + run("relu", 3, 4, 8) + [("rbcopy", 0)] + run("cast", 2, 0, 4) + run("sq", 1, 3, 8)
+        act = act + run("sq", 2, 0, 4) + [("root", 1)] + run("sq", 2, 4, 8) + run("sq", 3, 0, 2) + run("cast", 3, 4, 6) + [("root", 2)] + run("cast", 3, 6, 8) + run("sq", 3, 2, 4)
+        act = act + [("rbcopy", 2)] + run("sq", 3, 4, 8) + [("root", 3)]
+
+        dve = [("n",), ("scale", 0, 0), ("scale", 0, 1)]
+        for j in range(1, TILES):
+            dve = dve + [("scale", j, 0), ("xq", j - 1), ("scale", j, 1)]
+        dve = dve + [("xq", 7), ("mred", 0)]
+        dve = dve + run("centre", 0, 0, 7) + run("cast", 0, 0, 4) + [("mred", 1)] + il(0, 0) + run("centre", 0, 7, 8) + [("q", 0, 0)]
+        dve = dve + run("centre", 1, 0, 7) + [("mred", 2), ("q", 0, 1)] + il(1, 0) + run("centre", 1, 7, 8) + [("q", 1, 0)]
+        dve = dve + run("centre", 2, 0, 3) + [("vred", 0)] + run("centre", 2, 3, 5) + [("recip", 0)] + run("centre", 2, 5, 7) + [("q", 1, 1), ("mred", 3)] + il(2, 0) + run("centre", 2, 7, 8) + [("q", 2, 0)]
+        dve = dve + run("centre", 3, 0, 3) + [("vred", 1), ("q", 2, 1)] + run("centre", 3, 3, 8) + [("recip", 1), ("vred", 2)] + each("fin", 0, 2) + [("recip", 2)] + each("fin", 2, 4)
+        dve = dve + [("q", 3, 0)] + il(3, 1) + each("fin", 4, 5) + [("q", 3, 1)] + each("fin", 5, 6) + [("vred", 3)] + each("fin", 6, 7) + [("recip", 3)] + each("fin", 7, 16)
+        pool = [("pool", c, g) for c, g in ON_POOL]
+
+        queues = [pe, act, dve, pool]
+        assert sorted(pe + act + dve + pool) == sorted(steps)
+        done = set()
+        heads = [0] * len(queues)
+        while len(done) < len(steps):
+            moved = False
+            for e, queue in enumerate(queues):
+                if heads[e] < len(queue) and steps[queue[heads[e]]][1] <= done:
+                    steps[queue[heads[e]]][0]()
+                    done.add(queue[heads[e]])
+                    heads[e] = heads[e] + 1
+                    moved = True
+            assert moved

@@ -25,10 +25,12 @@ TILES = 8
 FB = CH // P
 FLOPS = 3 * 2 * 1024 * 1024 * 1024
 
-ON_POOL = [(0, 1), (1, 1), (2, 1), (3, 0)]
-CAST_V = [(0, 0), (0, 1), (0, 2), (0, 3)]
-IL_S = []
-OUT_BANKS = [2, 3, 4, 5, 6, 1, 2, 3, 4, 5, 6, 1, 0, 2, 3, 7]
+ON_POOL = [(0, 1), (1, 1), (2, 1), (3, 1)]
+CAST_V = [(c, j) for c in (0, 2) for j in range(4)]
+IL_S = [(3, 0, 0)]
+WIDEN_V = 2
+VAR_BANKS = [7, 7, 2, 7]
+OUT_BANKS = [3, 4, 5, 1, 3, 4, 5, 1, 0, 2, 3, 4, 5, 1, 6, 7]
 CHUNKS = [(1, 0), (0, 0), (1, 1), (0, 1)]
 
 
@@ -49,7 +51,7 @@ def tile_zipitweightedfeaturecorrelation_w4_kernel(
         mean_banks = [banks[1], banks[0]]
         h_banks = banks[2:6]
         macc = banks[6]
-        vacc = banks[7]
+        vacc = [banks[b] for b in VAR_BANKS]
 
         ident = sbt("ident", [P, P], F32)
         p_sb = sbt("p_sb", [P, 2, 4], BF16)
@@ -84,7 +86,6 @@ def tile_zipitweightedfeaturecorrelation_w4_kernel(
         vroot = [sbt("vroot%d" % c, [P, FB], F32) for c in range(4)]
         rinv = [sbt("rinv%d" % c, [P, FB], F32) for c in range(4)]
         rb_rows = [sbt("rb_rows%d" % h, [P, CH], F32) for h in range(2)]
-        ostage = [sbt("ostage%d" % i, [P, CH], F32) for i in range(8)]
 
         words_in = [wa_words, wb_words]
         scales_in = [wa_scales, wb_scales]
@@ -126,24 +127,33 @@ def tile_zipitweightedfeaturecorrelation_w4_kernel(
         q_flat = q_sb[:].rearrange("p g t -> p (g t)")
         nc.vector.tensor_tensor(out=t_sb[:], in0=p_flat, in1=q_flat, op=ALU.mult)
         nc.scalar.activation(out=root_t[:], in_=t_sb[:], func=ACT.Sqrt)
-        nc.vector.reciprocal(out=inv_other[0][:], in_=q_flat)
-        nc.vector.reciprocal(out=inv_other[1][:], in_=p_flat)
-        nc.vector.tensor_reduce(out=t_row[:], in_=t_sb[:], axis=AX.X, op=ALU.add)
-        nc.vector.reciprocal(out=rroot_t[:], in_=root_t[:])
+
+        def weights_inverses():
+            nc.vector.tensor_reduce(out=t_row[:], in_=t_sb[:], axis=AX.X, op=ALU.add)
+            nc.vector.reciprocal(out=inv_other[0][:], in_=q_flat)
+            nc.vector.reciprocal(out=inv_other[1][:], in_=p_flat)
+            nc.vector.reciprocal(out=rroot_t[:], in_=root_t[:])
 
         def spread(bank, col0, column):
             nc.tensor.transpose(bank[:, col0 : col0 + P], column.to_broadcast([P, P]), ident[:])
 
-        def weights_n():
+        def sum_n():
             nc.vector.tensor_reduce(out=n_sb[:], in_=macc[:, 0:P], axis=AX.X, op=ALU.add)
+
+        def invert_n():
             nc.vector.reciprocal(out=inv_n[:], in_=n_sb[:])
+
+        def centring_factor():
             nc.vector.tensor_scalar(
                 out=neg_tn[:], in0=t_sb[:], scalar1=inv_n[:, 0:1], scalar2=-1.0, op0=ALU.mult, op1=ALU.mult
             )
 
         def widen_x(j):
             i, r = xsrc[j]
-            nc.scalar.copy(out=xwide[j][:], in_=xraw[i][:, r, :].bitcast(FP8))
+            if j < WIDEN_V:
+                nc.vector.tensor_copy(out=xwide[j][:], in_=xraw[i][:, r, :].bitcast(FP8))
+            else:
+                nc.scalar.copy(out=xwide[j][:], in_=xraw[i][:, r, :].bitcast(FP8))
 
         def turn_x(j):
             words = xwide[j][:].bitcast(F32)
@@ -253,19 +263,19 @@ def tile_zipitweightedfeaturecorrelation_w4_kernel(
 
         def finish(bank, i, ca, f, cb):
             ha, hb = CHUNKS[ca][1], CHUNKS[cb][1]
-            st = ostage[i % 8]
+            st = th[i // TILES][i % TILES]
             nc.vector.scalar_tensor_tensor(
-                out=st[:], in0=bank[:], scalar=rinv[ca][:, f : f + 1], in1=rb_rows[hb][:],
+                out=st, in0=bank[:], scalar=rinv[ca][:, f : f + 1], in1=rb_rows[hb][:],
                 op0=ALU.mult, op1=ALU.mult,
             )
             row = ha * CH + f * P
-            nc.sync.dma_start(out=out[row : row + P, hb * CH : (hb + 1) * CH], in_=st[:])
+            nc.sync.dma_start(out=out[row : row + P, hb * CH : (hb + 1) * CH], in_=st)
 
         def mean_sum(c, j):
             add_turned(macc, th[c][j], j)
 
         def var_sum(c, j):
-            add_turned(vacc, sq[(c % 2) * TILES + j][:], j)
+            add_turned(vacc[c], sq[(c % 2) * TILES + j][:], j)
 
         def spread_mean(c):
             for f in range(FB):
@@ -273,10 +283,10 @@ def tile_zipitweightedfeaturecorrelation_w4_kernel(
 
         def spread_rb(c):
             for f in range(FB):
-                spread(vacc, f * P, rinv[c][:, f : f + 1])
+                spread(macc, f * P, rinv[c][:, f : f + 1])
 
         def copy_rb(c):
-            nc.scalar.copy(out=rb_rows[CHUNKS[c][1]][:], in_=vacc[:])
+            nc.scalar.copy(out=rb_rows[CHUNKS[c][1]][:], in_=macc[:])
 
         def recip(c):
             nc.vector.reciprocal(out=rinv[c][:], in_=vroot[c][:])
@@ -299,8 +309,11 @@ def tile_zipitweightedfeaturecorrelation_w4_kernel(
             steps[key] = (call, after - {key})
 
         x_bank_no = [0, 1, 7]
-        step(("spread_t",), lambda: spread(macc, 0, t_row[:, 0:1]), [], [("bank", 6)])
-        step(("n",), weights_n, [("bank", 6)], ["n"])
+        step(("inv",), weights_inverses, [], ["inv"])
+        step(("spread_t",), partial(spread, macc, 0, t_row[:, 0:1]), ["inv"], [("bank", 6)])
+        step(("n", 0), sum_n, [("bank", 6)], ["n0"])
+        step(("n", 1), invert_n, ["n0"], ["n1"])
+        step(("n", 2), centring_factor, ["n1"], ["n"])
         for j in range(TILES):
             xb = ("bank", x_bank_no[j % 3])
             step(("widen", j), partial(widen_x, j), [], [("xwide", j)])
@@ -318,11 +331,12 @@ def tile_zipitweightedfeaturecorrelation_w4_kernel(
                 step(("relu", c, j), partial(relu_out, c, j), [hb], [("th", c, j)])
                 step(("msum", c, j), partial(mean_sum, c, j), [("th", c, j)], [("bank", 6)])
             step(("mred", c), partial(sum_tokens, msum[c], macc), [("bank", 6)], [("m", c)])
+        for c in range(4):
             step(("mspread", c), partial(spread_mean, c), [("m", c)], [("bank", 1 - c % 2)])
             for j in range(TILES):
                 step(("centre", c, j), partial(centre, c, j), [("bank", 1 - c % 2), "n"], [("th", c, j)])
                 step(("sq", c, j), partial(square, c, j), [("th", c, j)], [("sq", c % 2, j)])
-                step(("vsum", c, j), partial(var_sum, c, j), [("sq", c % 2, j)], [("bank", 7)])
+                step(("vsum", c, j), partial(var_sum, c, j), [("sq", c % 2, j)], [("bank", VAR_BANKS[c])])
             for g in range(2):
                 group = [("th", c, j) for j in range(4 * g, 4 * g + 4)]
                 if (c, g) in ON_POOL:
@@ -334,19 +348,19 @@ def tile_zipitweightedfeaturecorrelation_w4_kernel(
                         step(("il", c, g, h), partial(interleave, c, g, h),
                              [("plane", j) for j in range(4 * g, 4 * g + 4)], [("inter", c % 2, g, h)])
                 step(("q", c, g), partial(quant, c, g), [("inter", c % 2, g, h) for h in range(2)], [("codes", c, g)])
-            step(("vred", c), partial(sum_tokens, vsum[c], vacc), [("bank", 7)], [("v", c)])
+            step(("vred", c), partial(sum_tokens, vsum[c], vacc[c]), [("bank", VAR_BANKS[c])], [("v", c)])
             step(("root", c), partial(norm_root, c), [("v", c)], [("root", c)])
             step(("recip", c), partial(recip, c), [("root", c)], [("rinv", c)])
-            if CHUNKS[c][0] == 1:
-                step(("rbspread", c), partial(spread_rb, c), [("rinv", c)], [("bank", 7)])
-                step(("rbcopy", c), partial(copy_rb, c), [("bank", 7)], [("rb", c)])
+        for c in (0, 2):
+            step(("rbspread", c), partial(spread_rb, c), [("rinv", c)], [("bank", 6)])
+            step(("rbcopy", c), partial(copy_rb, c), [("bank", 6)], [("rb", c)])
         for c in range(1, 4):
             for ca, f, cb in out_tiles[c]:
                 ob = OUT_BANKS[n_out]
                 needs = [("codes", k, g) for k in (ca, cb) for g in range(2)]
                 step(("mx2", n_out), partial(second_product, banks[ob], ca, f, cb), needs, [("bank", ob)])
                 step(("fin", n_out), partial(finish, banks[ob], n_out, ca, f, cb),
-                     [("bank", ob), ("rinv", ca), ("rb", cb)], [("ostage", n_out % 8)])
+                     [("bank", ob), ("rinv", ca), ("rb", cb)], [("th",) + divmod(n_out, TILES)])
                 n_out = n_out + 1
 
         def run(name, c, lo, hi):
@@ -358,31 +372,31 @@ def tile_zipitweightedfeaturecorrelation_w4_kernel(
         def il(c, g):
             return [("il", c, g, 0), ("il", c, g, 1)]
 
-        pe = [("spread_t",)] + each("turn", 0, 3) + run("mx", 0, 0, 1) + each("turn", 3, 5) + run("mx", 0, 1, 3)
-        pe = pe + each("turn", 5, 7) + run("mx", 0, 3, 4) + each("turn", 7, 8) + run("msum", 0, 0, 3) + run("mx", 0, 4, 7)
-        pe = pe + run("msum", 0, 3, 6) + run("mx", 0, 7, 8) + run("mx", 1, 0, 1) + run("msum", 0, 6, 8) + run("mx", 1, 1, 4)
-        pe = pe + [("mspread", 0)] + run("msum", 1, 0, 4) + run("mx", 1, 4, 8) + run("msum", 1, 4, 8)
-        pe = pe + run("mx", 2, 0, 4) + [("mspread", 1)] + run("msum", 2, 0, 4) + run("mx", 2, 4, 8) + run("vsum", 0, 0, 2) + run("msum", 2, 4, 8)
-        pe = pe + run("mx", 3, 0, 4) + [("mspread", 2)] + run("vsum", 0, 2, 8) + run("msum", 3, 0, 4) + run("mx", 3, 4, 8) + [("rbspread", 0)] + run("msum", 3, 4, 8)
-        pe = pe + run("vsum", 1, 0, 4) + [("mspread", 3)] + run("vsum", 1, 4, 8) + each("mx2", 0, 4) + run("vsum", 2, 0, 8)
-        pe = pe + [("rbspread", 2)] + each("mx2", 4, 8) + run("vsum", 3, 0, 8) + each("mx2", 8, 16)
+        pe = each("turn", 0, 2) + [("spread_t",)] + each("turn", 2, 4)
+        for j in range(4):
+            pe = pe + [("mx", 0, j), ("turn", j + 4)] + run("msum", 0, max(j - 2, 0), max(j - 1, 0))
+        pe = pe + run("mx", 0, 4, 6) + run("msum", 0, 2, 4) + run("mx", 0, 6, 7) + run("msum", 0, 4, 6) + run("mx", 0, 7, 8) + run("mx", 1, 0, 1) + run("msum", 0, 6, 8)
+        pe = pe + run("mx", 1, 1, 3) + [("mspread", 0)] + run("mx", 1, 3, 8) + run("msum", 1, 0, 8) + run("vsum", 0, 0, 4) + [("mspread", 1)]
+        pe = pe + run("mx", 2, 0, 8) + run("msum", 2, 0, 8) + run("vsum", 0, 4, 8) + [("mspread", 2)]
+        pe = pe + run("mx", 3, 0, 8) + run("msum", 3, 0, 8) + run("vsum", 1, 0, 4) + [("mspread", 3)]
+        pe = pe + [("rbspread", 0)] + run("vsum", 1, 4, 8) + run("vsum", 2, 0, 8) + each("mx2", 0, 4)
+        pe = pe + run("vsum", 3, 0, 2) + [("rbspread", 2)] + each("mx2", 4, 8) + run("vsum", 3, 2, 8) + each("mx2", 8, 16)
 
-        act = each("widen", 0, 7) + run("relu", 0, 0, 1) + each("widen", 7, 8) + run("relu", 0, 1, 8) + run("relu", 1, 0, 4)
-        act = act + run("sq", 0, 0, 2) + run("relu", 1, 4, 8) + run("sq", 0, 2, 4) + run("relu", 2, 0, 4) + run("sq", 0, 4, 7)
-        act = act + run("relu", 2, 4, 8) + run("cast", 1, 0, 4) + run("sq", 0, 7, 8) + run("relu", 3, 0, 4) + run("sq", 1, 0, 3) + [("root", 0)]
-        act = act + run("relu", 3, 4, 8) + [("rbcopy", 0)] + run("cast", 2, 0, 4) + run("sq", 1, 3, 8)
-        act = act + run("sq", 2, 0, 4) + [("root", 1)] + run("sq", 2, 4, 8) + run("sq", 3, 0, 2) + run("cast", 3, 4, 6) + [("root", 2)] + run("cast", 3, 6, 8) + run("sq", 3, 2, 4)
-        act = act + [("rbcopy", 2)] + run("sq", 3, 4, 8) + [("root", 3)]
+        act = each("widen", 2, 7) + run("relu", 0, 0, 1) + each("widen", 7, 8) + run("relu", 0, 1, 8)
+        act = act + run("relu", 1, 0, 8) + run("sq", 0, 0, 7)
+        act = act + run("relu", 2, 0, 8) + run("sq", 0, 7, 8) + run("cast", 1, 0, 4) + run("sq", 1, 0, 2)
+        act = act + run("relu", 3, 0, 8) + run("sq", 1, 2, 4) + [("root", 0)] + run("sq", 1, 4, 8) + run("sq", 2, 0, 2) + [("rbcopy", 0)] + run("sq", 2, 2, 8)
+        act = act + run("cast", 3, 0, 4) + [("root", 1)] + run("sq", 3, 0, 2) + [("root", 2), ("il", 3, 0, 0), ("rbcopy", 2)] + run("sq", 3, 2, 8) + [("root", 3)]
 
-        dve = [("n",), ("scale", 0, 0), ("scale", 0, 1)]
+        dve = each("widen", 0, 2) + [("inv",), ("scale", 0, 0), ("scale", 0, 1)]
         for j in range(1, TILES):
-            dve = dve + [("scale", j, 0), ("xq", j - 1), ("scale", j, 1)]
+            dve = dve + [("scale", j, 0), ("xq", j - 1), ("scale", j, 1)] + each("n", j - 1, min(j, 3))
         dve = dve + [("xq", 7), ("mred", 0)]
         dve = dve + run("centre", 0, 0, 7) + run("cast", 0, 0, 4) + [("mred", 1)] + il(0, 0) + run("centre", 0, 7, 8) + [("q", 0, 0)]
-        dve = dve + run("centre", 1, 0, 7) + [("mred", 2), ("q", 0, 1)] + il(1, 0) + run("centre", 1, 7, 8) + [("q", 1, 0)]
-        dve = dve + run("centre", 2, 0, 3) + [("vred", 0)] + run("centre", 2, 3, 5) + [("recip", 0)] + run("centre", 2, 5, 7) + [("q", 1, 1), ("mred", 3)] + il(2, 0) + run("centre", 2, 7, 8) + [("q", 2, 0)]
-        dve = dve + run("centre", 3, 0, 3) + [("vred", 1), ("q", 2, 1)] + run("centre", 3, 3, 8) + [("recip", 1), ("vred", 2)] + each("fin", 0, 2) + [("recip", 2)] + each("fin", 2, 4)
-        dve = dve + [("q", 3, 0)] + il(3, 1) + each("fin", 4, 5) + [("q", 3, 1)] + each("fin", 5, 6) + [("vred", 3)] + each("fin", 6, 7) + [("recip", 3)] + each("fin", 7, 16)
+        dve = dve + run("centre", 1, 0, 7) + [("q", 0, 1), ("mred", 2)] + il(1, 0) + run("centre", 1, 7, 8) + [("q", 1, 0)]
+        dve = dve + run("centre", 2, 0, 4) + [("vred", 0)] + run("centre", 2, 4, 7) + run("cast", 2, 0, 4) + [("recip", 0), ("mred", 3)] + il(2, 0) + [("q", 1, 1)] + run("centre", 2, 7, 8) + [("q", 2, 0)]
+        dve = dve + run("centre", 3, 0, 7) + [("vred", 1), ("q", 2, 1)] + run("centre", 3, 7, 8) + [("recip", 1), ("vred", 2)]
+        dve = dve + each("fin", 0, 1) + [("recip", 2)] + each("fin", 1, 7) + [("il", 3, 0, 1), ("q", 3, 1), ("q", 3, 0), ("vred", 3)] + each("fin", 7, 8) + [("recip", 3)] + each("fin", 8, 16)
         pool = [("pool", c, g) for c, g in ON_POOL]
 
         queues = [pe, act, dve, pool]

@@ -25,9 +25,10 @@ TILES = 8
 FB = CH // P
 FLOPS = 3 * 2 * 1024 * 1024 * 1024
 
-ON_POOL = [(0, 1), (1, 1), (2, 1), (3, 1)]
-CAST_V = [(c, j) for c in (0, 2) for j in range(4)]
-IL_S = [(3, 0, 0)]
+ON_POOL = [(0, 0), (0, 1), (1, 1), (2, 1), (3, 1)]
+CAST_V = [(c, j) for c in (1, 2) for j in range(4)]
+IL_S = [(3, 0, 0), (3, 0, 1)]
+RELU_V = [(1, 6), (1, 7)]
 WIDEN_V = 2
 VAR_BANKS = [7, 7, 2, 7]
 OUT_BANKS = [3, 4, 5, 1, 3, 4, 5, 1, 0, 2, 3, 4, 5, 1, 6, 7]
@@ -125,8 +126,12 @@ def tile_zipitweightedfeaturecorrelation_w4_kernel(
 
         p_flat = p_sb[:].rearrange("p g t -> p (g t)")
         q_flat = q_sb[:].rearrange("p g t -> p (g t)")
-        nc.vector.tensor_tensor(out=t_sb[:], in0=p_flat, in1=q_flat, op=ALU.mult)
-        nc.scalar.activation(out=root_t[:], in_=t_sb[:], func=ACT.Sqrt)
+
+        def token_weights():
+            nc.vector.tensor_tensor(out=t_sb[:], in0=p_flat, in1=q_flat, op=ALU.mult)
+
+        def root_of_weights():
+            nc.scalar.activation(out=root_t[:], in_=t_sb[:], func=ACT.Sqrt)
 
         def weights_inverses():
             nc.vector.tensor_reduce(out=t_row[:], in_=t_sb[:], axis=AX.X, op=ALU.add)
@@ -187,7 +192,13 @@ def tile_zipitweightedfeaturecorrelation_w4_kernel(
                 )
 
         def relu_out(c, j):
-            nc.scalar.activation(out=th[c][j], in_=h_banks[j % 4][:], func=ACT.Relu, scale=t_sb[:, j : j + 1])
+            if (c, j) in RELU_V:
+                nc.vector.tensor_scalar(
+                    out=th[c][j], in0=h_banks[j % 4][:], scalar1=0.0, scalar2=t_sb[:, j : j + 1],
+                    op0=ALU.max, op1=ALU.mult,
+                )
+            else:
+                nc.scalar.activation(out=th[c][j], in_=h_banks[j % 4][:], func=ACT.Relu, scale=t_sb[:, j : j + 1])
 
         def add_turned(acc, src, j):
             for f in range(FB):
@@ -309,7 +320,9 @@ def tile_zipitweightedfeaturecorrelation_w4_kernel(
             steps[key] = (call, after - {key})
 
         x_bank_no = [0, 1, 7]
-        step(("inv",), weights_inverses, [], ["inv"])
+        step(("t",), token_weights, [], ["t"])
+        step(("root_t",), root_of_weights, ["t"], ["root_t"])
+        step(("inv",), weights_inverses, ["root_t"], ["inv"])
         step(("spread_t",), partial(spread, macc, 0, t_row[:, 0:1]), ["inv"], [("bank", 6)])
         step(("n", 0), sum_n, [("bank", 6)], ["n0"])
         step(("n", 1), invert_n, ["n0"], ["n1"])
@@ -328,7 +341,7 @@ def tile_zipitweightedfeaturecorrelation_w4_kernel(
             for j in range(TILES):
                 hb = ("bank", 2 + j % 4)
                 step(("mx", c, j), partial(first_product, c, j), [("xc", j)], [hb])
-                step(("relu", c, j), partial(relu_out, c, j), [hb], [("th", c, j)])
+                step(("relu", c, j), partial(relu_out, c, j), [hb, "t"], [("th", c, j)])
                 step(("msum", c, j), partial(mean_sum, c, j), [("th", c, j)], [("bank", 6)])
             step(("mred", c), partial(sum_tokens, msum[c], macc), [("bank", 6)], [("m", c)])
         for c in range(4):
@@ -380,23 +393,23 @@ def tile_zipitweightedfeaturecorrelation_w4_kernel(
         pe = pe + run("mx", 2, 0, 8) + run("msum", 2, 0, 8) + run("vsum", 0, 4, 8) + [("mspread", 2)]
         pe = pe + run("mx", 3, 0, 8) + run("msum", 3, 0, 8) + run("vsum", 1, 0, 4) + [("mspread", 3)]
         pe = pe + [("rbspread", 0)] + run("vsum", 1, 4, 8) + run("vsum", 2, 0, 8) + each("mx2", 0, 4)
-        pe = pe + run("vsum", 3, 0, 2) + [("rbspread", 2)] + each("mx2", 4, 8) + run("vsum", 3, 2, 8) + each("mx2", 8, 16)
+        pe = pe + run("vsum", 3, 0, 7) + [("rbspread", 2)] + run("vsum", 3, 7, 8) + each("mx2", 4, 8) + each("mx2", 8, 16)
 
-        act = each("widen", 2, 7) + run("relu", 0, 0, 1) + each("widen", 7, 8) + run("relu", 0, 1, 8)
-        act = act + run("relu", 1, 0, 8) + run("sq", 0, 0, 7)
-        act = act + run("relu", 2, 0, 8) + run("sq", 0, 7, 8) + run("cast", 1, 0, 4) + run("sq", 1, 0, 2)
-        act = act + run("relu", 3, 0, 8) + run("sq", 1, 2, 4) + [("root", 0)] + run("sq", 1, 4, 8) + run("sq", 2, 0, 2) + [("rbcopy", 0)] + run("sq", 2, 2, 8)
-        act = act + run("cast", 3, 0, 4) + [("root", 1)] + run("sq", 3, 0, 2) + [("root", 2), ("il", 3, 0, 0), ("rbcopy", 2)] + run("sq", 3, 2, 8) + [("root", 3)]
+        act = [("root_t",)] + each("widen", 2, 7) + run("relu", 0, 0, 1) + each("widen", 7, 8) + run("relu", 0, 1, 8)
+        act = act + run("relu", 1, 0, 6) + run("sq", 0, 0, 8)
+        act = act + run("relu", 2, 0, 8) + run("sq", 1, 0, 7)
+        act = act + run("relu", 3, 0, 8) + run("sq", 1, 7, 8) + [("root", 0)] + run("sq", 2, 0, 5) + [("rbcopy", 0)] + run("sq", 2, 5, 8)
+        act = act + run("cast", 3, 0, 4) + run("sq", 3, 0, 3) + [("root", 1)] + run("sq", 3, 3, 7) + [("root", 2)] + run("sq", 3, 7, 8) + [("il", 3, 0, 0), ("rbcopy", 2), ("root", 3), ("il", 3, 0, 1)]
 
-        dve = each("widen", 0, 2) + [("inv",), ("scale", 0, 0), ("scale", 0, 1)]
+        dve = [("widen", 0), ("t",), ("widen", 1), ("inv",), ("scale", 0, 0), ("scale", 0, 1)]
         for j in range(1, TILES):
             dve = dve + [("scale", j, 0), ("xq", j - 1), ("scale", j, 1)] + each("n", j - 1, min(j, 3))
         dve = dve + [("xq", 7), ("mred", 0)]
-        dve = dve + run("centre", 0, 0, 7) + run("cast", 0, 0, 4) + [("mred", 1)] + il(0, 0) + run("centre", 0, 7, 8) + [("q", 0, 0)]
-        dve = dve + run("centre", 1, 0, 7) + [("q", 0, 1), ("mred", 2)] + il(1, 0) + run("centre", 1, 7, 8) + [("q", 1, 0)]
-        dve = dve + run("centre", 2, 0, 4) + [("vred", 0)] + run("centre", 2, 4, 7) + run("cast", 2, 0, 4) + [("recip", 0), ("mred", 3)] + il(2, 0) + [("q", 1, 1)] + run("centre", 2, 7, 8) + [("q", 2, 0)]
+        dve = dve + run("centre", 0, 0, 4) + run("relu", 1, 6, 8) + run("centre", 0, 4, 8) + [("mred", 1)]
+        dve = dve + run("centre", 1, 0, 7) + run("cast", 1, 0, 4) + [("q", 0, 0)] + il(1, 0) + [("mred", 2)] + run("centre", 1, 7, 8)
+        dve = dve + run("centre", 2, 0, 7) + [("vred", 0)] + run("cast", 2, 0, 4) + [("q", 0, 1), ("q", 1, 0), ("recip", 0), ("mred", 3), ("q", 1, 1)] + il(2, 0) + run("centre", 2, 7, 8) + [("q", 2, 0)]
         dve = dve + run("centre", 3, 0, 7) + [("vred", 1), ("q", 2, 1)] + run("centre", 3, 7, 8) + [("recip", 1), ("vred", 2)]
-        dve = dve + each("fin", 0, 1) + [("recip", 2)] + each("fin", 1, 7) + [("il", 3, 0, 1), ("q", 3, 1), ("q", 3, 0), ("vred", 3)] + each("fin", 7, 8) + [("recip", 3)] + each("fin", 8, 16)
+        dve = dve + each("fin", 0, 1) + [("recip", 2)] + each("fin", 1, 4) + [("vred", 3)] + each("fin", 4, 6) + [("recip", 3), ("q", 3, 1), ("q", 3, 0)] + each("fin", 6, 8) + each("fin", 8, 16)
         pool = [("pool", c, g) for c, g in ON_POOL]
 
         queues = [pe, act, dve, pool]

@@ -17,115 +17,127 @@ ACT = mybir.ActivationFunctionType
 AX = mybir.AxisListType
 
 P = 128
-N_TOK = 1024
+PACK = 4
+PASSES = 2
 D_IN = 1024
 N_FEAT = 1024
 CH = 512
-TILES = 8
-FB = CH // P
+TILES = PASSES * PACK
+BLOCKS = CH // P
 FLOPS = 3 * 2 * 1024 * 1024 * 1024
 
-ON_POOL = [(0, 0), (0, 1), (1, 1), (2, 1), (3, 1)]
-CAST_V = [(c, j) for c in (1, 2) for j in range(4)]
-IL_S = [(3, 0, 0), (3, 0, 1)]
-RELU_V = [(1, 6), (1, 7)]
-WIDEN_V = 2
+MODEL_A = 0
+MODEL_B = 1
+CHUNKS = [(MODEL_B, 0), (MODEL_A, 0), (MODEL_B, 1), (MODEL_A, 1)]
+OUT_TILES = [(1, f, 0) for f in range(BLOCKS)] + [(1, f, 2) for f in range(BLOCKS)]
+OUT_TILES = OUT_TILES + [(3, f, cb) for f in range(BLOCKS) for cb in (0, 2)]
+
+X_BANKS = [0, 1, 7]
+H_BANKS = [2, 3, 4, 5]
+SUM_BANK = 6
+MEAN_BANKS = [1, 0]
 VAR_BANKS = [7, 7, 2, 7]
 OUT_BANKS = [3, 4, 5, 1, 3, 4, 5, 1, 0, 2, 3, 4, 5, 1, 6, 7]
-CHUNKS = [(1, 0), (0, 0), (1, 1), (0, 1)]
+
+WIDEN_ON_VECTOR = 2
+RELU_ON_VECTOR = [(1, 6), (1, 7)]
+POOL_GROUPS = [(0, 0), (0, 1), (1, 1), (2, 1), (3, 1)]
+SCALAR_GROUP = (3, 0)
+INTER_BUFFER = [[0, 1], [2, 1], [3, 1], [0, 1]]
 
 
 def tile_zipitweightedfeaturecorrelation_w4_kernel(
     tc, x_bytes, x_scale, wa_words, wa_scales, wb_words, wb_scales, p, q, out
 ):
     nc = tc.nc
+    n_chunks = len(CHUNKS)
     with ExitStack() as ctx:
         sb = ctx.enter_context(tc.tile_pool(name="sb", bufs=1))
         ps = ctx.enter_context(tc.psum_pool(name="ps", bufs=1))
         ctx.enter_context(tc.manual_schedule())
 
-        def sbt(name, shape, dtype):
+        def sbuf(name, shape, dtype):
             return sb.tile(shape, dtype, name=name, align_bytes=64)
 
         banks = [ps.tile([P, CH], F32, name="bank%d" % i) for i in range(8)]
-        x_banks = [banks[0], banks[1], banks[7]]
-        mean_banks = [banks[1], banks[0]]
-        h_banks = banks[2:6]
-        macc = banks[6]
-        vacc = [banks[b] for b in VAR_BANKS]
+        sum_bank = banks[SUM_BANK]
 
-        ident = sbt("ident", [P, P], F32)
-        p_sb = sbt("p_sb", [P, 2, 4], BF16)
-        q_sb = sbt("q_sb", [P, 2, 4], BF16)
-        xs_sb = sbt("xs_sb", [P, 2, 4], F32)
-        xraw = [sbt("xraw0", [P, 1, D_IN], U8), sbt("xraw1", [P, 1, D_IN], U8),
-                sbt("xraw2", [P, 2, D_IN], U8), sbt("xraw3", [P, 4, D_IN], U8)]
-        xsrc = [(0, 0), (1, 0), (2, 0), (2, 1), (3, 0), (3, 1), (3, 2), (3, 3)]
-        xwide = [sbt("xwide%d" % i, [P, D_IN], BF16) for i in range(TILES)]
-        xil = [sbt("xil%d" % i, [P, D_IN], BF16) for i in range(4)]
-        xcodes = [sbt("xcodes%d" % i, [P, 2 * P], U32) for i in range(TILES)]
-        xscales = [sbt("xscales%d" % i, [P, 2 * P], U8) for i in range(TILES)]
-        wwords = [sbt("wwords%d" % c, [P, 2, 2 * CH], U8) for c in range(4)]
-        wscales = [sbt("wscales%d" % m, [P, 2, N_FEAT], U8) for m in range(2)]
-        th4 = [[sbt("th%d_%d" % (c, g), [P, 4, CH], F32) for g in range(2)] for c in range(4)]
-        th = [[th4[c][j // 4][:, j % 4, :] for j in range(TILES)] for c in range(4)]
-        sq = [sbt("sq%d" % i, [P, CH], F32) for i in range(2 * TILES)]
-        planes = [sbt("planes%d" % i, [P, 4, CH], BF16) for i in range(2)]
-        inter = [sbt("inter%d" % i, [P, 4 * CH], BF16) for i in range(4)]
-        codes = [[sbt("codes%d_%d" % (c, g), [P, CH], U32) for g in range(2)] for c in range(4)]
-        cscales = [[sbt("cscales%d_%d" % (c, g), [P, CH], U8) for g in range(2)] for c in range(4)]
-        t_sb = sbt("t_sb", [P, TILES], F32)
-        root_t = sbt("root_t", [P, TILES], F32)
-        rroot_t = sbt("rroot_t", [P, TILES], F32)
-        inv_other = [sbt("inv_q", [P, TILES], F32), sbt("inv_p", [P, TILES], F32)]
-        t_row = sbt("t_row", [P, 1], F32)
-        n_sb = sbt("n_sb", [P, 1], F32)
-        inv_n = sbt("inv_n", [P, 1], F32)
-        neg_tn = sbt("neg_tn", [P, TILES], F32)
-        msum = [sbt("msum%d" % c, [P, FB], F32) for c in range(4)]
-        vsum = [sbt("vsum%d" % c, [P, FB], F32) for c in range(4)]
-        vroot = [sbt("vroot%d" % c, [P, FB], F32) for c in range(4)]
-        rinv = [sbt("rinv%d" % c, [P, FB], F32) for c in range(4)]
-        rb_rows = [sbt("rb_rows%d" % h, [P, CH], F32) for h in range(2)]
+        ident = sbuf("ident", [P, P], F32)
+        p_sb = sbuf("p_sb", [P, PASSES, PACK], BF16)
+        q_sb = sbuf("q_sb", [P, PASSES, PACK], BF16)
+        xs_sb = sbuf("xs_sb", [P, PASSES, PACK], F32)
+        x_loads = [(0, 1), (1, 2), (2, 4), (4, 8)]
+        xraw = [sbuf("xraw%d" % i, [P, hi - lo, D_IN], U8) for i, (lo, hi) in enumerate(x_loads)]
+        xraw_tile = [xraw[i][:, j - lo, :] for i, (lo, hi) in enumerate(x_loads) for j in range(lo, hi)]
+        xwide = [sbuf("xwide%d" % j, [P, D_IN], BF16) for j in range(TILES)]
+        xinter = [sbuf("xinter%d" % i, [P, D_IN], BF16) for i in range(4)]
+        xcodes = [sbuf("xcodes%d" % j, [P, PASSES * P], U32) for j in range(TILES)]
+        xscales = [sbuf("xscales%d" % j, [P, PASSES * P], U8) for j in range(TILES)]
+        wwords = [sbuf("wwords%d" % c, [P, PASSES, 2 * CH], U8) for c in range(n_chunks)]
+        wscales = [sbuf("wscales%d" % m, [P, PASSES, N_FEAT], U8) for m in range(2)]
+        feat_group = [
+            [sbuf("feat%d_%d" % (c, g), [P, PACK, CH], F32) for g in range(PASSES)] for c in range(n_chunks)
+        ]
+        feat = [[feat_group[c][j // PACK][:, j % PACK, :] for j in range(TILES)] for c in range(n_chunks)]
+        squares = [sbuf("squares%d" % i, [P, CH], F32) for i in range(2 * TILES)]
+        cast_group = sbuf("cast_group", [P, PACK, CH], BF16)
+        inter = [sbuf("inter%d" % i, [P, PACK * CH], BF16) for i in range(4)]
+        codes = [[sbuf("codes%d_%d" % (c, g), [P, CH], U32) for g in range(PASSES)] for c in range(n_chunks)]
+        cscales = [[sbuf("cscales%d_%d" % (c, g), [P, CH], U8) for g in range(PASSES)] for c in range(n_chunks)]
+        t_sb = sbuf("t_sb", [P, TILES], F32)
+        root_t = sbuf("root_t", [P, TILES], F32)
+        inv_root_t = sbuf("inv_root_t", [P, TILES], F32)
+        inv_other = [sbuf("inv_q", [P, TILES], F32), sbuf("inv_p", [P, TILES], F32)]
+        t_row = sbuf("t_row", [P, 1], F32)
+        n_sb = sbuf("n_sb", [P, 1], F32)
+        inv_n = sbuf("inv_n", [P, 1], F32)
+        neg_t_over_n = sbuf("neg_t_over_n", [P, TILES], F32)
+        th_sum = [sbuf("th_sum%d" % c, [P, BLOCKS], F32) for c in range(n_chunks)]
+        var = [sbuf("var%d" % c, [P, BLOCKS], F32) for c in range(n_chunks)]
+        std = [sbuf("std%d" % c, [P, BLOCKS], F32) for c in range(n_chunks)]
+        inv_std = [sbuf("inv_std%d" % c, [P, BLOCKS], F32) for c in range(n_chunks)]
+        inv_std_rows = [sbuf("inv_std_rows%d" % h, [P, CH], F32) for h in range(2)]
 
-        words_in = [wa_words, wb_words]
-        scales_in = [wa_scales, wb_scales]
-
-        nc.scalar.dma_start(out=p_sb[:], in_=p.rearrange("(g m t) -> m g t", g=2, t=4))
-        nc.scalar.dma_start(out=q_sb[:], in_=q.rearrange("(g m t) -> m g t", g=2, t=4))
-        nc.scalar.dma_start(out=xs_sb[:], in_=x_scale.rearrange("o (g m t) -> m (o g) t", g=2, t=4))
-        for m in (1, 0):
+        nc.scalar.dma_start(out=p_sb[:], in_=p.rearrange("(g m s) -> m g s", g=PASSES, s=PACK))
+        nc.scalar.dma_start(out=q_sb[:], in_=q.rearrange("(g m s) -> m g s", g=PASSES, s=PACK))
+        nc.scalar.dma_start(out=xs_sb[:], in_=x_scale.rearrange("o (g m s) -> m (o g) s", g=PASSES, s=PACK))
+        for m in (MODEL_B, MODEL_A):
             nc.vector.memset(wscales[m][:].rearrange("p g n -> p (g n)").bitcast(I32), 0)
         make_identity(nc, ident[:])
 
-        x_rows = x_bytes.rearrange("(g m t) k -> g m t k", g=2, t=4)
+        x_rows = x_bytes.rearrange("(g m s) k -> g m s k", g=PASSES, s=PACK)
+
+        def load_x(i):
+            lo, hi = x_loads[i]
+            g = lo // PACK
+            nc.sync.dma_start(out=xraw[i][:], in_=x_rows[g][:, lo - PACK * g : hi - PACK * g, :])
 
         def load_words(c):
             m, h = CHUNKS[c]
+            words = [wa_words, wb_words][m].rearrange("g p n -> p g n")
             nc.sync.dma_start(
-                out=wwords[c][:].bitcast(I32),
-                in_=words_in[m].rearrange("g p n -> p g n")[:, :, 2 * CH * h : 2 * CH * (h + 1)].bitcast(I32),
+                out=wwords[c][:].bitcast(I32), in_=words[:, :, 2 * CH * h : 2 * CH * (h + 1)].bitcast(I32)
             )
 
         def load_scales(m):
+            rows = [wa_scales, wb_scales][m].rearrange("g r n -> r g n")
             for quad in range(4):
                 nc.sync.dma_start(
                     out=wscales[m][32 * quad : 32 * quad + 4, :, :].bitcast(I32),
-                    in_=scales_in[m].rearrange("g r n -> r g n")[4 * quad : 4 * quad + 4, :, :].bitcast(I32),
+                    in_=rows[4 * quad : 4 * quad + 4, :, :].bitcast(I32),
                 )
 
-        nc.sync.dma_start(out=xraw[0][:], in_=x_rows[0][:, 0:1, :])
-        nc.sync.dma_start(out=xraw[1][:], in_=x_rows[0][:, 1:2, :])
-        nc.sync.dma_start(out=xraw[2][:], in_=x_rows[0][:, 2:4, :])
-        load_scales(1)
+        for i in range(3):
+            load_x(i)
+        load_scales(MODEL_B)
         load_words(0)
-        nc.sync.dma_start(out=xraw[3][:], in_=x_rows[1])
-        load_scales(0)
-        for c in range(1, 4):
+        load_x(3)
+        load_scales(MODEL_A)
+        for c in range(1, n_chunks):
             load_words(c)
 
-        p_flat = p_sb[:].rearrange("p g t -> p (g t)")
-        q_flat = q_sb[:].rearrange("p g t -> p (g t)")
+        p_flat = p_sb[:].rearrange("p g s -> p (g s)")
+        q_flat = q_sb[:].rearrange("p g s -> p (g s)")
 
         def token_weights():
             nc.vector.tensor_tensor(out=t_sb[:], in0=p_flat, in1=q_flat, op=ALU.mult)
@@ -133,284 +145,279 @@ def tile_zipitweightedfeaturecorrelation_w4_kernel(
         def root_of_weights():
             nc.scalar.activation(out=root_t[:], in_=t_sb[:], func=ACT.Sqrt)
 
-        def weights_inverses():
+        def weight_inverses():
             nc.vector.tensor_reduce(out=t_row[:], in_=t_sb[:], axis=AX.X, op=ALU.add)
-            nc.vector.reciprocal(out=inv_other[0][:], in_=q_flat)
-            nc.vector.reciprocal(out=inv_other[1][:], in_=p_flat)
-            nc.vector.reciprocal(out=rroot_t[:], in_=root_t[:])
+            nc.vector.reciprocal(out=inv_other[MODEL_A][:], in_=q_flat)
+            nc.vector.reciprocal(out=inv_other[MODEL_B][:], in_=p_flat)
+            nc.vector.reciprocal(out=inv_root_t[:], in_=root_t[:])
 
-        def spread(bank, col0, column):
-            nc.tensor.transpose(bank[:, col0 : col0 + P], column.to_broadcast([P, P]), ident[:])
+        def spread(bank, columns):
+            for f in range(columns.shape[1]):
+                nc.tensor.transpose(
+                    bank[:, f * P : (f + 1) * P], columns[:, f : f + 1].to_broadcast([P, P]), ident[:]
+                )
 
         def sum_n():
-            nc.vector.tensor_reduce(out=n_sb[:], in_=macc[:, 0:P], axis=AX.X, op=ALU.add)
+            nc.vector.tensor_reduce(out=n_sb[:], in_=sum_bank[:, 0:P], axis=AX.X, op=ALU.add)
 
         def invert_n():
             nc.vector.reciprocal(out=inv_n[:], in_=n_sb[:])
 
         def centring_factor():
             nc.vector.tensor_scalar(
-                out=neg_tn[:], in0=t_sb[:], scalar1=inv_n[:, 0:1], scalar2=-1.0, op0=ALU.mult, op1=ALU.mult
+                out=neg_t_over_n[:], in0=t_sb[:], scalar1=inv_n[:, 0:1], scalar2=-1.0, op0=ALU.mult, op1=ALU.mult
             )
 
         def widen_x(j):
-            i, r = xsrc[j]
-            if j < WIDEN_V:
-                nc.vector.tensor_copy(out=xwide[j][:], in_=xraw[i][:, r, :].bitcast(FP8))
+            if j < WIDEN_ON_VECTOR:
+                nc.vector.tensor_copy(out=xwide[j][:], in_=xraw_tile[j].bitcast(FP8))
             else:
-                nc.scalar.copy(out=xwide[j][:], in_=xraw[i][:, r, :].bitcast(FP8))
+                nc.scalar.copy(out=xwide[j][:], in_=xraw_tile[j].bitcast(FP8))
 
         def turn_x(j):
             words = xwide[j][:].bitcast(F32)
-            for g in range(2):
+            bank = banks[X_BANKS[j % 3]]
+            for g in range(PASSES):
                 for u in range(2):
                     col = (2 * g + u) * P
-                    nc.tensor.transpose(
-                        x_banks[j % 3][:, col : col + P], words[:, 256 * g + u : 256 * (g + 1) : 2], ident[:]
-                    )
+                    nc.tensor.transpose(bank[:, col : col + P], words[:, 256 * g + u : 256 * (g + 1) : 2], ident[:])
 
         def scale_x(j, g):
-            src = x_banks[j % 3][:].bitcast(BF16).rearrange("p (g u r e) -> p g r u e", g=2, u=2, e=2)
-            dst = xil[j % 4][:].rearrange("p (g r u e) -> p g r u e", g=2, u=2, e=2)
-            sc = xs_sb[:, g, :].rearrange("p (u e) -> p u e", u=2).unsqueeze(1).to_broadcast([P, P, 2, 2])
-            nc.vector.tensor_tensor(out=dst[:, g, :, :, :], in0=src[:, g, :, :, :], in1=sc, op=ALU.mult)
+            src = banks[X_BANKS[j % 3]][:].bitcast(BF16).rearrange("p (g u r e) -> p g r u e", g=PASSES, u=2, e=2)
+            dst = xinter[j % 4][:].rearrange("p (g r u e) -> p g r u e", g=PASSES, u=2, e=2)
+            factor = xs_sb[:, g, :].rearrange("p (u e) -> p u e", u=2).unsqueeze(1).to_broadcast([P, P, 2, 2])
+            nc.vector.tensor_tensor(out=dst[:, g, :, :, :], in0=src[:, g, :, :, :], in1=factor, op=ALU.mult)
 
-        def quant_x(j):
-            nc.vector.quantize_mx(out=xcodes[j][:].bitcast(FP8X4), scales=xscales[j][:], in_=xil[j % 4][:])
+        def quantise_x(j):
+            nc.vector.quantize_mx(out=xcodes[j][:].bitcast(FP8X4), scales=xscales[j][:], in_=xinter[j % 4][:])
 
         def first_product(c, j):
             m, h = CHUNKS[c]
-            for g in range(2):
+            for g in range(PASSES):
                 nc.tensor.matmul_mx(
-                    out=h_banks[j % 4][:],
+                    out=banks[H_BANKS[j % 4]][:],
                     lhsT=xcodes[j][:, g * P : (g + 1) * P].bitcast(FP8X4),
                     lhsT_scale=xscales[j][:, g * P : (g + 1) * P],
                     rhs=wwords[c][:, g, :].bitcast(FP4X4),
                     rhs_scale=wscales[m][:, g, h * CH : (h + 1) * CH],
                     start=(g == 0),
-                    stop=(g == 1),
+                    stop=(g == PASSES - 1),
                 )
 
-        def relu_out(c, j):
-            if (c, j) in RELU_V:
+        def weighted_relu(c, j):
+            bank = banks[H_BANKS[j % 4]]
+            if (c, j) in RELU_ON_VECTOR:
                 nc.vector.tensor_scalar(
-                    out=th[c][j], in0=h_banks[j % 4][:], scalar1=0.0, scalar2=t_sb[:, j : j + 1],
-                    op0=ALU.max, op1=ALU.mult,
+                    out=feat[c][j], in0=bank[:], scalar1=0.0, scalar2=t_sb[:, j : j + 1], op0=ALU.max, op1=ALU.mult
                 )
             else:
-                nc.scalar.activation(out=th[c][j], in_=h_banks[j % 4][:], func=ACT.Relu, scale=t_sb[:, j : j + 1])
+                nc.scalar.activation(out=feat[c][j], in_=bank[:], func=ACT.Relu, scale=t_sb[:, j : j + 1])
 
-        def add_turned(acc, src, j):
-            for f in range(FB):
+        def add_turned(bank, src, j):
+            for f in range(BLOCKS):
                 nc.tensor.matmul(
-                    out=acc[:, f * P : (f + 1) * P],
+                    out=bank[:, f * P : (f + 1) * P],
                     lhsT=src[:, f * P : (f + 1) * P],
                     rhs=ident[:],
                     is_transpose=True,
                     start=(j == 0 and f == 0),
-                    stop=(j == TILES - 1 and f == FB - 1),
+                    stop=(j == TILES - 1 and f == BLOCKS - 1),
                 )
 
-        def sum_tokens(dst, acc):
+        def sum_tokens(dst, bank):
             nc.vector.tensor_reduce(
-                out=dst[:], in_=acc[:].rearrange("p (f m) -> p f m", f=FB), axis=AX.X, op=ALU.add
+                out=dst[:], in_=bank[:].rearrange("p (f m) -> p f m", f=BLOCKS), axis=AX.X, op=ALU.add
             )
 
         def centre(c, j):
             nc.vector.scalar_tensor_tensor(
-                out=th[c][j], in0=mean_banks[c % 2][:], scalar=neg_tn[:, j : j + 1], in1=th[c][j],
+                out=feat[c][j], in0=banks[MEAN_BANKS[c % 2]][:], scalar=neg_t_over_n[:, j : j + 1], in1=feat[c][j],
                 op0=ALU.mult, op1=ALU.add,
             )
 
         def square(c, j):
             nc.scalar.activation(
-                out=sq[(c % 2) * TILES + j][:], in_=th[c][j], func=ACT.Square, scale=rroot_t[:, j : j + 1]
+                out=squares[(c % 2) * TILES + j][:], in_=feat[c][j], func=ACT.Square, scale=inv_root_t[:, j : j + 1]
             )
 
-        def cast(c, j, on_vector):
-            inv = inv_other[CHUNKS[c][0]][:, j : j + 1]
-            dst = planes[j // 4][:, j % 4, :]
-            if on_vector:
-                nc.vector.tensor_scalar(out=dst, in0=th[c][j], scalar1=inv, scalar2=None, op0=ALU.mult)
+        def cast(c, j):
+            factor = inv_other[CHUNKS[c][0]][:, j : j + 1]
+            if (c, j // PACK) == SCALAR_GROUP:
+                nc.scalar.activation(out=cast_group[:, j % PACK, :], in_=feat[c][j], func=ACT.Copy, scale=factor)
             else:
-                nc.scalar.activation(out=dst, in_=th[c][j], func=ACT.Copy, scale=inv)
+                nc.vector.tensor_scalar(
+                    out=cast_group[:, j % PACK, :], in0=feat[c][j], scalar1=factor, scalar2=None, op0=ALU.mult
+                )
 
-        def interleave(c, g, h):
-            half = CH // 2
-            dst = inter[(c % 2) * 2 + g][:, 4 * half * h : 4 * half * (h + 1)].rearrange("p (c i t) -> p c t i", i=4, t=4)
-            src = planes[g][:, :, half * h : half * (h + 1)].rearrange("p t (c i) -> p c t i", i=4)
-            if (c, g, h) in IL_S:
+        def interleave(c, g):
+            dst = inter[INTER_BUFFER[c][g]][:].rearrange("p (a i s) -> p a s i", i=4, s=PACK)
+            src = cast_group[:].rearrange("p s (a i) -> p a s i", i=4)
+            if (c, g) == SCALAR_GROUP:
                 nc.scalar.copy(out=dst, in_=src)
             else:
                 nc.vector.tensor_copy(out=dst, in_=src)
 
-        def scale_interleave(c, g):
-            inv = inv_other[CHUNKS[c][0]][:, 4 * g : 4 * g + 4].unsqueeze(1).to_broadcast([P, CH, 4])
+        def scale_and_interleave(c, g):
+            factor = inv_other[CHUNKS[c][0]][:, PACK * g : PACK * (g + 1)].unsqueeze(1).to_broadcast([P, CH, PACK])
             nc.gpsimd.tensor_tensor(
-                out=inter[(c % 2) * 2 + g][:].rearrange("p (f t) -> p f t", t=4),
-                in0=th4[c][g][:].rearrange("p t f -> p f t"),
-                in1=inv,
+                out=inter[INTER_BUFFER[c][g]][:].rearrange("p (f s) -> p f s", s=PACK),
+                in0=feat_group[c][g][:].rearrange("p s f -> p f s"),
+                in1=factor,
                 op=ALU.mult,
             )
 
-        def quant(c, g):
-            nc.vector.quantize_mx(out=codes[c][g][:].bitcast(FP8X4), scales=cscales[c][g][:], in_=inter[(c % 2) * 2 + g][:])
+        def quantise(c, g):
+            nc.vector.quantize_mx(
+                out=codes[c][g][:].bitcast(FP8X4), scales=cscales[c][g][:], in_=inter[INTER_BUFFER[c][g]][:]
+            )
 
-        def norm_root(c):
-            scale = 1.0 / 1024.0 if CHUNKS[c][0] == 0 else 1.0
-            nc.scalar.activation(out=vroot[c][:], in_=vsum[c][:], func=ACT.Sqrt, scale=scale)
+        def root_of_var(c):
+            scale = 1.0 / 1024.0 if CHUNKS[c][0] == MODEL_A else 1.0
+            nc.scalar.activation(out=std[c][:], in_=var[c][:], func=ACT.Sqrt, scale=scale)
 
-        def second_product(bank, ca, f, cb):
-            for g in range(2):
+        def invert_std(c):
+            nc.vector.reciprocal(out=inv_std[c][:], in_=std[c][:])
+
+        def copy_inv_std_rows(c):
+            nc.scalar.copy(out=inv_std_rows[CHUNKS[c][1]][:], in_=sum_bank[:])
+
+        def second_product(k):
+            ca, f, cb = OUT_TILES[k]
+            for g in range(PASSES):
                 nc.tensor.matmul_mx(
-                    out=bank[:],
+                    out=banks[OUT_BANKS[k]][:],
                     lhsT=codes[ca][g][:, f * P : (f + 1) * P].bitcast(FP8X4),
                     lhsT_scale=cscales[ca][g][:, f * P : (f + 1) * P],
                     rhs=codes[cb][g][:].bitcast(FP8X4),
                     rhs_scale=cscales[cb][g][:],
                     start=(g == 0),
-                    stop=(g == 1),
+                    stop=(g == PASSES - 1),
                 )
 
-        def finish(bank, i, ca, f, cb):
-            ha, hb = CHUNKS[ca][1], CHUNKS[cb][1]
-            st = th[i // TILES][i % TILES]
+        def finish(k):
+            ca, f, cb = OUT_TILES[k]
+            stage = feat[k // TILES][k % TILES]
             nc.vector.scalar_tensor_tensor(
-                out=st, in0=bank[:], scalar=rinv[ca][:, f : f + 1], in1=rb_rows[hb][:],
-                op0=ALU.mult, op1=ALU.mult,
+                out=stage, in0=banks[OUT_BANKS[k]][:], scalar=inv_std[ca][:, f : f + 1],
+                in1=inv_std_rows[CHUNKS[cb][1]][:], op0=ALU.mult, op1=ALU.mult,
             )
-            row = ha * CH + f * P
-            nc.sync.dma_start(out=out[row : row + P, hb * CH : (hb + 1) * CH], in_=st)
-
-        def mean_sum(c, j):
-            add_turned(macc, th[c][j], j)
-
-        def var_sum(c, j):
-            add_turned(vacc[c], sq[(c % 2) * TILES + j][:], j)
-
-        def spread_mean(c):
-            for f in range(FB):
-                spread(mean_banks[c % 2], f * P, msum[c][:, f : f + 1])
-
-        def spread_rb(c):
-            for f in range(FB):
-                spread(macc, f * P, rinv[c][:, f : f + 1])
-
-        def copy_rb(c):
-            nc.scalar.copy(out=rb_rows[CHUNKS[c][1]][:], in_=macc[:])
-
-        def recip(c):
-            nc.vector.reciprocal(out=rinv[c][:], in_=vroot[c][:])
+            row = CHUNKS[ca][1] * CH + f * P
+            col = CHUNKS[cb][1] * CH
+            nc.sync.dma_start(out=out[row : row + P, col : col + CH], in_=stage)
 
         steps = {}
-        last_write = {}
+        last_writer = {}
         readers = {}
 
         def step(key, call, reads, writes):
-            after = set()
-            for r in reads + writes:
-                if r in last_write:
-                    after.add(last_write[r])
+            after = set(last_writer[r] for r in reads + writes if r in last_writer)
             for w in writes:
                 after = after | set(readers.get(w, []))
                 readers[w] = []
-                last_write[w] = key
+                last_writer[w] = key
             for r in reads:
                 readers.setdefault(r, []).append(key)
-            steps[key] = (call, after - {key})
+            steps[key] = (call, after)
 
-        x_bank_no = [0, 1, 7]
         step(("t",), token_weights, [], ["t"])
         step(("root_t",), root_of_weights, ["t"], ["root_t"])
-        step(("inv",), weights_inverses, ["root_t"], ["inv"])
-        step(("spread_t",), partial(spread, macc, 0, t_row[:, 0:1]), ["inv"], [("bank", 6)])
-        step(("n", 0), sum_n, [("bank", 6)], ["n0"])
-        step(("n", 1), invert_n, ["n0"], ["n1"])
-        step(("n", 2), centring_factor, ["n1"], ["n"])
+        step(("inverses",), weight_inverses, ["root_t"], ["inverses"])
+        step(("spread_t",), partial(spread, sum_bank, t_row[:]), ["inverses"], [("bank", SUM_BANK)])
+        step(("n", 0), sum_n, [("bank", SUM_BANK)], ["n"])
+        step(("n", 1), invert_n, ["n"], ["inv_n"])
+        step(("n", 2), centring_factor, ["inv_n"], ["t_over_n"])
         for j in range(TILES):
-            xb = ("bank", x_bank_no[j % 3])
+            x_bank = ("bank", X_BANKS[j % 3])
             step(("widen", j), partial(widen_x, j), [], [("xwide", j)])
-            step(("turn", j), partial(turn_x, j), [("xwide", j)], [xb])
-            for g in range(2):
-                step(("scale", j, g), partial(scale_x, j, g), [xb], [("xil", j % 4, g)])
-            step(("xq", j), partial(quant_x, j), [("xil", j % 4, 0), ("xil", j % 4, 1)], [("xc", j)])
-        out_tiles = {1: [(1, f, 0) for f in range(FB)], 2: [(1, f, 2) for f in range(FB)],
-                     3: [(3, f, cb) for f in range(FB) for cb in (0, 2)]}
-        n_out = 0
-        for c in range(4):
+            step(("turn", j), partial(turn_x, j), [("xwide", j)], [x_bank])
+            for g in range(PASSES):
+                step(("scale", j, g), partial(scale_x, j, g), [x_bank], [("xinter", j % 4, g)])
+            step(("xquant", j), partial(quantise_x, j), [("xinter", j % 4, g) for g in range(PASSES)], [("xcodes", j)])
+        for c in range(n_chunks):
             for j in range(TILES):
-                hb = ("bank", 2 + j % 4)
-                step(("mx", c, j), partial(first_product, c, j), [("xc", j)], [hb])
-                step(("relu", c, j), partial(relu_out, c, j), [hb, "t"], [("th", c, j)])
-                step(("msum", c, j), partial(mean_sum, c, j), [("th", c, j)], [("bank", 6)])
-            step(("mred", c), partial(sum_tokens, msum[c], macc), [("bank", 6)], [("m", c)])
-        for c in range(4):
-            step(("mspread", c), partial(spread_mean, c), [("m", c)], [("bank", 1 - c % 2)])
+                h_bank = ("bank", H_BANKS[j % 4])
+                step(("mx1", c, j), partial(first_product, c, j), [("xcodes", j)], [h_bank])
+                step(("relu", c, j), partial(weighted_relu, c, j), [h_bank, "t"], [("feat", c, j)])
+                step(("add_th", c, j), partial(add_turned, sum_bank, feat[c][j], j), [("feat", c, j)],
+                     [("bank", SUM_BANK)])
+            step(("sum_th", c), partial(sum_tokens, th_sum[c], sum_bank), [("bank", SUM_BANK)], [("th_sum", c)])
+        for c in range(n_chunks):
+            mean_bank = ("bank", MEAN_BANKS[c % 2])
+            var_bank = ("bank", VAR_BANKS[c])
+            step(("spread_th", c), partial(spread, banks[MEAN_BANKS[c % 2]], th_sum[c][:]), [("th_sum", c)],
+                 [mean_bank])
             for j in range(TILES):
-                step(("centre", c, j), partial(centre, c, j), [("bank", 1 - c % 2), "n"], [("th", c, j)])
-                step(("sq", c, j), partial(square, c, j), [("th", c, j)], [("sq", c % 2, j)])
-                step(("vsum", c, j), partial(var_sum, c, j), [("sq", c % 2, j)], [("bank", VAR_BANKS[c])])
-            for g in range(2):
-                group = [("th", c, j) for j in range(4 * g, 4 * g + 4)]
-                if (c, g) in ON_POOL:
-                    step(("pool", c, g), partial(scale_interleave, c, g), group, [("inter", c % 2, g, h) for h in range(2)])
+                step(("centre", c, j), partial(centre, c, j), [mean_bank, "t_over_n"], [("feat", c, j)])
+                step(("square", c, j), partial(square, c, j), [("feat", c, j)], [("squares", c % 2, j)])
+                step(("add_sq", c, j), partial(add_turned, banks[VAR_BANKS[c]], squares[(c % 2) * TILES + j][:], j),
+                     [("squares", c % 2, j)], [var_bank])
+            for g in range(PASSES):
+                tiles = range(PACK * g, PACK * (g + 1))
+                buffer = ("inter", INTER_BUFFER[c][g])
+                if (c, g) in POOL_GROUPS:
+                    step(("pool", c, g), partial(scale_and_interleave, c, g), [("feat", c, j) for j in tiles], [buffer])
                 else:
-                    for j in range(4 * g, 4 * g + 4):
-                        step(("cast", c, j), partial(cast, c, j, (c, j) in CAST_V), [("th", c, j)], [("plane", j)])
-                    for h in range(2):
-                        step(("il", c, g, h), partial(interleave, c, g, h),
-                             [("plane", j) for j in range(4 * g, 4 * g + 4)], [("inter", c % 2, g, h)])
-                step(("q", c, g), partial(quant, c, g), [("inter", c % 2, g, h) for h in range(2)], [("codes", c, g)])
-            step(("vred", c), partial(sum_tokens, vsum[c], vacc[c]), [("bank", VAR_BANKS[c])], [("v", c)])
-            step(("root", c), partial(norm_root, c), [("v", c)], [("root", c)])
-            step(("recip", c), partial(recip, c), [("root", c)], [("rinv", c)])
-        for c in (0, 2):
-            step(("rbspread", c), partial(spread_rb, c), [("rinv", c)], [("bank", 6)])
-            step(("rbcopy", c), partial(copy_rb, c), [("bank", 6)], [("rb", c)])
-        for c in range(1, 4):
-            for ca, f, cb in out_tiles[c]:
-                ob = OUT_BANKS[n_out]
-                needs = [("codes", k, g) for k in (ca, cb) for g in range(2)]
-                step(("mx2", n_out), partial(second_product, banks[ob], ca, f, cb), needs, [("bank", ob)])
-                step(("fin", n_out), partial(finish, banks[ob], n_out, ca, f, cb),
-                     [("bank", ob), ("rinv", ca), ("rb", cb)], [("th",) + divmod(n_out, TILES)])
-                n_out = n_out + 1
+                    for j in tiles:
+                        step(("cast", c, j), partial(cast, c, j), [("feat", c, j)], [("cast", j % PACK)])
+                    step(("inter", c, g), partial(interleave, c, g), [("cast", s) for s in range(PACK)], [buffer])
+                step(("quant", c, g), partial(quantise, c, g), [buffer], [("codes", c, g)])
+            step(("sum_sq", c), partial(sum_tokens, var[c], banks[VAR_BANKS[c]]), [var_bank], [("var", c)])
+            step(("root", c), partial(root_of_var, c), [("var", c)], [("std", c)])
+            step(("invert", c), partial(invert_std, c), [("std", c)], [("inv_std", c)])
+        for c in range(n_chunks):
+            if CHUNKS[c][0] == MODEL_B:
+                step(("spread_std", c), partial(spread, sum_bank, inv_std[c][:]), [("inv_std", c)],
+                     [("bank", SUM_BANK)])
+                step(("rows", c), partial(copy_inv_std_rows, c), [("bank", SUM_BANK)], [("rows", c)])
+        for k, (ca, f, cb) in enumerate(OUT_TILES):
+            out_bank = ("bank", OUT_BANKS[k])
+            step(("mx2", k), partial(second_product, k), [("codes", c, g) for c in (ca, cb) for g in range(PASSES)],
+                 [out_bank])
+            step(("finish", k), partial(finish, k), [out_bank, ("inv_std", ca), ("rows", cb)],
+                 [("feat",) + divmod(k, TILES)])
 
-        def run(name, c, lo, hi):
+        def run(name, c, lo=0, hi=TILES):
             return [(name, c, j) for j in range(lo, hi)]
 
         def each(name, lo, hi):
             return [(name, k) for k in range(lo, hi)]
 
-        def il(c, g):
-            return [("il", c, g, 0), ("il", c, g, 1)]
-
         pe = each("turn", 0, 2) + [("spread_t",)] + each("turn", 2, 4)
         for j in range(4):
-            pe = pe + [("mx", 0, j), ("turn", j + 4)] + run("msum", 0, max(j - 2, 0), max(j - 1, 0))
-        pe = pe + run("mx", 0, 4, 6) + run("msum", 0, 2, 4) + run("mx", 0, 6, 7) + run("msum", 0, 4, 6) + run("mx", 0, 7, 8) + run("mx", 1, 0, 1) + run("msum", 0, 6, 8)
-        pe = pe + run("mx", 1, 1, 3) + [("mspread", 0)] + run("mx", 1, 3, 8) + run("msum", 1, 0, 8) + run("vsum", 0, 0, 4) + [("mspread", 1)]
-        pe = pe + run("mx", 2, 0, 8) + run("msum", 2, 0, 8) + run("vsum", 0, 4, 8) + [("mspread", 2)]
-        pe = pe + run("mx", 3, 0, 8) + run("msum", 3, 0, 8) + run("vsum", 1, 0, 4) + [("mspread", 3)]
-        pe = pe + [("rbspread", 0)] + run("vsum", 1, 4, 8) + run("vsum", 2, 0, 8) + each("mx2", 0, 4)
-        pe = pe + run("vsum", 3, 0, 7) + [("rbspread", 2)] + run("vsum", 3, 7, 8) + each("mx2", 4, 8) + each("mx2", 8, 16)
+            pe = pe + [("mx1", 0, j), ("turn", j + 4)] + run("add_th", 0, max(j - 2, 0), max(j - 1, 0))
+        pe = pe + run("mx1", 0, 4, 6) + run("add_th", 0, 2, 4) + run("mx1", 0, 6, 7) + run("add_th", 0, 4, 6)
+        pe = pe + run("mx1", 0, 7) + run("mx1", 1, 0, 1) + run("add_th", 0, 6) + run("mx1", 1, 1, 3)
+        pe = pe + [("spread_th", 0)] + run("mx1", 1, 3)
+        pe = pe + run("add_th", 1) + run("add_sq", 0, 0, 4) + [("spread_th", 1)]
+        pe = pe + run("mx1", 2) + run("add_th", 2) + run("add_sq", 0, 4) + [("spread_th", 2)]
+        pe = pe + run("mx1", 3) + run("add_th", 3) + run("add_sq", 1, 0, 4) + [("spread_th", 3)]
+        pe = pe + [("spread_std", 0)] + run("add_sq", 1, 4) + run("add_sq", 2) + each("mx2", 0, 4)
+        pe = pe + run("add_sq", 3, 0, 5) + [("spread_std", 2)] + each("mx2", 4, 6) + run("add_sq", 3, 5)
+        pe = pe + each("mx2", 6, len(OUT_TILES))
 
-        act = [("root_t",)] + each("widen", 2, 7) + run("relu", 0, 0, 1) + each("widen", 7, 8) + run("relu", 0, 1, 8)
-        act = act + run("relu", 1, 0, 6) + run("sq", 0, 0, 8)
-        act = act + run("relu", 2, 0, 8) + run("sq", 1, 0, 7)
-        act = act + run("relu", 3, 0, 8) + run("sq", 1, 7, 8) + [("root", 0)] + run("sq", 2, 0, 5) + [("rbcopy", 0)] + run("sq", 2, 5, 8)
-        act = act + run("cast", 3, 0, 4) + run("sq", 3, 0, 3) + [("root", 1)] + run("sq", 3, 3, 7) + [("root", 2)] + run("sq", 3, 7, 8) + [("il", 3, 0, 0), ("rbcopy", 2), ("root", 3), ("il", 3, 0, 1)]
+        act = [("root_t",)] + each("widen", WIDEN_ON_VECTOR, 7) + run("relu", 0, 0, 1) + [("widen", 7)]
+        act = act + run("relu", 0, 1) + [key for key in run("relu", 1) if key[1:] not in RELU_ON_VECTOR]
+        act = act + run("square", 0) + run("relu", 2) + run("square", 1) + run("relu", 3)
+        act = act + [("root", 0)] + run("square", 2, 0, 5) + [("rows", 0)] + run("square", 2, 5)
+        act = act + run("cast", 3, 0, PACK) + run("square", 3, 0, 3) + [("root", 1)] + run("square", 3, 3, 5)
+        act = act + [("root", 2)] + run("square", 3, 5, 7) + [("rows", 2)] + run("square", 3, 7)
+        act = act + [("inter", 3, 0), ("root", 3)]
 
-        dve = [("widen", 0), ("t",), ("widen", 1), ("inv",), ("scale", 0, 0), ("scale", 0, 1)]
+        dve = [("widen", 0), ("t",), ("widen", 1), ("inverses",), ("scale", 0, 0), ("scale", 0, 1)]
         for j in range(1, TILES):
-            dve = dve + [("scale", j, 0), ("xq", j - 1), ("scale", j, 1)] + each("n", j - 1, min(j, 3))
-        dve = dve + [("xq", 7), ("mred", 0)]
-        dve = dve + run("centre", 0, 0, 4) + run("relu", 1, 6, 8) + run("centre", 0, 4, 8) + [("mred", 1)]
-        dve = dve + run("centre", 1, 0, 7) + run("cast", 1, 0, 4) + [("q", 0, 0)] + il(1, 0) + [("mred", 2)] + run("centre", 1, 7, 8)
-        dve = dve + run("centre", 2, 0, 7) + [("vred", 0)] + run("cast", 2, 0, 4) + [("q", 0, 1), ("q", 1, 0), ("recip", 0), ("mred", 3), ("q", 1, 1)] + il(2, 0) + run("centre", 2, 7, 8) + [("q", 2, 0)]
-        dve = dve + run("centre", 3, 0, 7) + [("vred", 1), ("q", 2, 1)] + run("centre", 3, 7, 8) + [("recip", 1), ("vred", 2)]
-        dve = dve + each("fin", 0, 1) + [("recip", 2)] + each("fin", 1, 4) + [("vred", 3)] + each("fin", 4, 6) + [("recip", 3), ("q", 3, 1), ("q", 3, 0)] + each("fin", 6, 8) + each("fin", 8, 16)
-        pool = [("pool", c, g) for c, g in ON_POOL]
+            dve = dve + [("scale", j, 0), ("xquant", j - 1), ("scale", j, 1)] + each("n", j - 1, min(j, 3))
+        dve = dve + [("xquant", TILES - 1), ("sum_th", 0)]
+        dve = dve + run("centre", 0, 0, 4) + [("relu",) + key for key in RELU_ON_VECTOR] + run("centre", 0, 4)
+        dve = dve + [("sum_th", 1)] + run("centre", 1)
+        dve = dve + run("cast", 1, 0, PACK) + [("quant", 0, 0), ("inter", 1, 0), ("sum_th", 2), ("quant", 0, 1)]
+        dve = dve + run("centre", 2, 0, 4) + [("sum_sq", 0)] + run("centre", 2, 4)
+        dve = dve + run("cast", 2, 0, PACK) + [("quant", 1, 0), ("invert", 0), ("sum_th", 3), ("inter", 2, 0)]
+        dve = dve + [("quant", 1, 1), ("quant", 2, 0)]
+        dve = dve + run("centre", 3) + [("sum_sq", 1), ("quant", 2, 1), ("sum_sq", 2), ("invert", 1)]
+        dve = dve + [("finish", 0), ("invert", 2)] + each("finish", 1, 6) + [("sum_sq", 3), ("finish", 6)]
+        dve = dve + [("quant", 3, 1), ("quant", 3, 0), ("invert", 3)] + each("finish", 7, len(OUT_TILES))
+
+        pool = [("pool", c, g) for c, g in POOL_GROUPS]
 
         queues = [pe, act, dve, pool]
         assert sorted(pe + act + dve + pool) == sorted(steps)

@@ -40,7 +40,9 @@ VAR_BANKS = [7, 7, 2, 7]
 OUT_BANKS = [3, 4, 5, 1, 3, 4, 5, 1, 0, 2, 3, 4, 5, 1, 6, 7]
 
 WIDEN_ON_VECTOR = 2
+PAIRED_CHUNKS = [0]
 RELU_ON_VECTOR = [(1, 6), (1, 7)]
+CAST_ON_VECTOR = 2
 POOL_GROUPS = [(0, 0), (0, 1), (1, 1), (2, 1), (3, 1)]
 SCALAR_GROUP = (3, 0)
 INTER_BUFFER = [[0, 1], [2, 1], [3, 1], [0, 1]]
@@ -213,15 +215,15 @@ def tile_zipitweightedfeaturecorrelation_w4_kernel(
             else:
                 nc.scalar.activation(out=feat[c][j], in_=bank[:], func=ACT.Relu, scale=t_sb[:, j : j + 1])
 
-        def add_turned(bank, src, j):
+        def add_turned(bank, src, first, last):
             for f in range(BLOCKS):
                 nc.tensor.matmul(
                     out=bank[:, f * P : (f + 1) * P],
                     lhsT=src[:, f * P : (f + 1) * P],
                     rhs=ident[:],
                     is_transpose=True,
-                    start=(j == 0 and f == 0),
-                    stop=(j == TILES - 1 and f == BLOCKS - 1),
+                    start=(first and f == 0),
+                    stop=(last and f == BLOCKS - 1),
                 )
 
         def sum_tokens(dst, bank):
@@ -242,12 +244,16 @@ def tile_zipitweightedfeaturecorrelation_w4_kernel(
 
         def cast(c, j):
             factor = inv_other[CHUNKS[c][0]][:, j : j + 1]
-            if (c, j // PACK) == SCALAR_GROUP:
-                nc.scalar.activation(out=cast_group[:, j % PACK, :], in_=feat[c][j], func=ACT.Copy, scale=factor)
-            else:
+            if c == CAST_ON_VECTOR:
                 nc.vector.tensor_scalar(
                     out=cast_group[:, j % PACK, :], in0=feat[c][j], scalar1=factor, scalar2=None, op0=ALU.mult
                 )
+            else:
+                nc.scalar.activation(out=cast_group[:, j % PACK, :], in_=feat[c][j], func=ACT.Copy, scale=factor)
+
+        def add_pair(c, j):
+            even, odd = squares[(c % 2) * TILES + j], squares[(c % 2) * TILES + j + 1]
+            nc.vector.tensor_tensor(out=even[:], in0=even[:], in1=odd[:], op=ALU.add)
 
         def interleave(c, g):
             dst = inter[INTER_BUFFER[c][g]][:].rearrange("p (a i s) -> p a s i", i=4, s=PACK)
@@ -338,8 +344,8 @@ def tile_zipitweightedfeaturecorrelation_w4_kernel(
                 h_bank = ("bank", H_BANKS[j % 4])
                 step(("mx1", c, j), partial(first_product, c, j), [("xcodes", j)], [h_bank])
                 step(("relu", c, j), partial(weighted_relu, c, j), [h_bank, "t"], [("feat", c, j)])
-                step(("add_th", c, j), partial(add_turned, sum_bank, feat[c][j], j), [("feat", c, j)],
-                     [("bank", SUM_BANK)])
+                step(("add_th", c, j), partial(add_turned, sum_bank, feat[c][j], j == 0, j == TILES - 1),
+                     [("feat", c, j)], [("bank", SUM_BANK)])
             step(("sum_th", c), partial(sum_tokens, th_sum[c], sum_bank), [("bank", SUM_BANK)], [("th_sum", c)])
         for c in range(n_chunks):
             mean_bank = ("bank", MEAN_BANKS[c % 2])
@@ -349,7 +355,12 @@ def tile_zipitweightedfeaturecorrelation_w4_kernel(
             for j in range(TILES):
                 step(("centre", c, j), partial(centre, c, j), [mean_bank, "t_over_n"], [("feat", c, j)])
                 step(("square", c, j), partial(square, c, j), [("feat", c, j)], [("squares", c % 2, j)])
-                step(("add_sq", c, j), partial(add_turned, banks[VAR_BANKS[c]], squares[(c % 2) * TILES + j][:], j),
+            added = range(0, TILES, 2) if c in PAIRED_CHUNKS else range(TILES)
+            for j in added:
+                if c in PAIRED_CHUNKS:
+                    step(("pair", c, j), partial(add_pair, c, j), [("squares", c % 2, j + 1)], [("squares", c % 2, j)])
+                src = squares[(c % 2) * TILES + j][:]
+                step(("add_sq", c, j), partial(add_turned, banks[VAR_BANKS[c]], src, j == added[0], j == added[-1]),
                      [("squares", c % 2, j)], [var_bank])
             for g in range(PASSES):
                 tiles = range(PACK * g, PACK * (g + 1))
@@ -379,6 +390,9 @@ def tile_zipitweightedfeaturecorrelation_w4_kernel(
         def run(name, c, lo=0, hi=TILES):
             return [(name, c, j) for j in range(lo, hi)]
 
+        def pairs(name, c):
+            return [(name, c, j) for j in range(0, TILES, 2)]
+
         def each(name, lo, hi):
             return [(name, k) for k in range(lo, hi)]
 
@@ -388,19 +402,20 @@ def tile_zipitweightedfeaturecorrelation_w4_kernel(
         pe = pe + run("mx1", 0, 4, 6) + run("add_th", 0, 2, 4) + run("mx1", 0, 6, 7) + run("add_th", 0, 4, 6)
         pe = pe + run("mx1", 0, 7) + run("mx1", 1, 0, 1) + run("add_th", 0, 6) + run("mx1", 1, 1, 3)
         pe = pe + [("spread_th", 0)] + run("mx1", 1, 3)
-        pe = pe + run("add_th", 1) + run("add_sq", 0, 0, 4) + [("spread_th", 1)]
-        pe = pe + run("mx1", 2) + run("add_th", 2) + run("add_sq", 0, 4) + [("spread_th", 2)]
+        pe = pe + run("add_th", 1) + run("mx1", 2, 0, 2) + [("spread_th", 1)] + run("mx1", 2, 2)
+        pe = pe + run("add_th", 2) + pairs("add_sq", 0) + [("spread_th", 2)]
         pe = pe + run("mx1", 3) + run("add_th", 3) + run("add_sq", 1, 0, 4) + [("spread_th", 3)]
-        pe = pe + [("spread_std", 0)] + run("add_sq", 1, 4) + run("add_sq", 2) + each("mx2", 0, 4)
-        pe = pe + run("add_sq", 3, 0, 5) + [("spread_std", 2)] + each("mx2", 4, 6) + run("add_sq", 3, 5)
+        pe = pe + run("add_sq", 1, 4) + [("spread_std", 0)] + run("add_sq", 2) + each("mx2", 0, 4)
+        pe = pe + run("add_sq", 3, 0, 4) + [("spread_std", 2)] + each("mx2", 4, 6) + run("add_sq", 3, 4)
         pe = pe + each("mx2", 6, len(OUT_TILES))
 
         act = [("root_t",)] + each("widen", WIDEN_ON_VECTOR, 7) + run("relu", 0, 0, 1) + [("widen", 7)]
         act = act + run("relu", 0, 1) + [key for key in run("relu", 1) if key[1:] not in RELU_ON_VECTOR]
-        act = act + run("square", 0) + run("relu", 2) + run("square", 1) + run("relu", 3)
-        act = act + [("root", 0)] + run("square", 2, 0, 5) + [("rows", 0)] + run("square", 2, 5)
-        act = act + run("cast", 3, 0, PACK) + run("square", 3, 0, 3) + [("root", 1)] + run("square", 3, 3, 5)
-        act = act + [("root", 2)] + run("square", 3, 5, 7) + [("rows", 2)] + run("square", 3, 7)
+        act = act + run("square", 0) + run("relu", 2) + run("cast", 1, 0, PACK) + run("square", 1, 0, 4)
+        act = act + run("relu", 3) + run("square", 1, 4)
+        act = act + [("root", 0)] + run("square", 2) + [("rows", 0)]
+        act = act + run("cast", 3, 0, PACK) + run("square", 3, 0, 2) + [("root", 1)] + run("square", 3, 2, 4)
+        act = act + [("root", 2)] + run("square", 3, 4, 7) + [("rows", 2)] + run("square", 3, 7)
         act = act + [("inter", 3, 0), ("root", 3)]
 
         dve = [("widen", 0), ("t",), ("widen", 1), ("inverses",), ("scale", 0, 0), ("scale", 0, 1)]
@@ -409,13 +424,13 @@ def tile_zipitweightedfeaturecorrelation_w4_kernel(
         dve = dve + [("xquant", TILES - 1), ("sum_th", 0)]
         dve = dve + run("centre", 0, 0, 4) + [("relu",) + key for key in RELU_ON_VECTOR] + run("centre", 0, 4)
         dve = dve + [("sum_th", 1)] + run("centre", 1)
-        dve = dve + run("cast", 1, 0, PACK) + [("quant", 0, 0), ("inter", 1, 0), ("sum_th", 2), ("quant", 0, 1)]
+        dve = dve + pairs("pair", 0) + [("sum_th", 2), ("inter", 1, 0), ("quant", 0, 0), ("quant", 0, 1)]
         dve = dve + run("centre", 2, 0, 4) + [("sum_sq", 0)] + run("centre", 2, 4)
-        dve = dve + run("cast", 2, 0, PACK) + [("quant", 1, 0), ("invert", 0), ("sum_th", 3), ("inter", 2, 0)]
+        dve = dve + run("cast", 2, 0, PACK) + [("quant", 1, 0), ("sum_th", 3), ("inter", 2, 0), ("invert", 0)]
         dve = dve + [("quant", 1, 1), ("quant", 2, 0)]
         dve = dve + run("centre", 3) + [("sum_sq", 1), ("quant", 2, 1), ("sum_sq", 2), ("invert", 1)]
-        dve = dve + [("finish", 0), ("invert", 2)] + each("finish", 1, 6) + [("sum_sq", 3), ("finish", 6)]
-        dve = dve + [("quant", 3, 1), ("quant", 3, 0), ("invert", 3)] + each("finish", 7, len(OUT_TILES))
+        dve = dve + [("finish", 0), ("invert", 2)] + each("finish", 1, 6) + [("quant", 3, 1), ("sum_sq", 3)]
+        dve = dve + [("quant", 3, 0), ("invert", 3)] + each("finish", 6, len(OUT_TILES))
 
         pool = [("pool", c, g) for c, g in POOL_GROUPS]
 

from contextlib import ExitStack
from functools import partial

import concourse.mybir as mybir
from concourse.masks import make_identity

F32 = mybir.dt.float32
BF16 = mybir.dt.bfloat16
I32 = mybir.dt.int32
U32 = mybir.dt.uint32
U8 = mybir.dt.uint8
FP8 = mybir.dt.float8_e4m3fn
FP8X4 = mybir.dt.float8_e4m3fn_x4
FP4X4 = mybir.dt.float4_e2m1fn_x4
ALU = mybir.AluOpType
ACT = mybir.ActivationFunctionType
AX = mybir.AxisListType

P = 128
PACK = 4
PASSES = 2
D_IN = 1024
N_FEAT = 1024
CH = 512
TILES = PASSES * PACK
BLOCKS = CH // P
FLOPS = 3 * 2 * 1024 * 1024 * 1024

MODEL_A = 0
MODEL_B = 1
CHUNKS = [(MODEL_B, 0), (MODEL_A, 0), (MODEL_B, 1), (MODEL_A, 1)]
OUT_TILES = [(1, f, 0) for f in range(BLOCKS)] + [(1, f, 2) for f in range(BLOCKS)]
OUT_TILES = OUT_TILES + [(3, f, cb) for f in range(BLOCKS) for cb in (0, 2)]

X_BANKS = [0, 1, 7]
H_BANKS = [2, 3, 4, 5]
SUM_BANK = 6
MEAN_BANKS = [1, 0]
VAR_BANKS = [7, 7, 2, 7]
OUT_BANKS = [3, 4, 5, 1, 3, 4, 5, 1, 0, 2, 3, 4, 5, 1, 6, 7]

WIDEN_ON_VECTOR = 2
PAIRED_CHUNKS = [0]
RELU_ON_VECTOR = [(1, 6), (1, 7)]
CAST_ON_VECTOR = 2
POOL_GROUPS = [(0, 0), (0, 1), (1, 1), (2, 1), (3, 1)]
SCALAR_GROUP = (3, 0)
INTER_BUFFER = [[0, 1], [2, 1], [3, 1], [0, 1]]


def tile_zipitweightedfeaturecorrelation_w4_kernel(
    tc, x_bytes, x_scale, wa_words, wa_scales, wb_words, wb_scales, p, q, out
):
    nc = tc.nc
    n_chunks = len(CHUNKS)
    with ExitStack() as ctx:
        sb = ctx.enter_context(tc.tile_pool(name="sb", bufs=1))
        ps = ctx.enter_context(tc.psum_pool(name="ps", bufs=1))
        ctx.enter_context(tc.manual_schedule())

        def sbuf(name, shape, dtype):
            return sb.tile(shape, dtype, name=name, align_bytes=64)

        banks = [ps.tile([P, CH], F32, name="bank%d" % i) for i in range(8)]
        sum_bank = banks[SUM_BANK]

        ident = sbuf("ident", [P, P], F32)
        p_sb = sbuf("p_sb", [P, PASSES, PACK], BF16)
        q_sb = sbuf("q_sb", [P, PASSES, PACK], BF16)
        xs_sb = sbuf("xs_sb", [P, PASSES, PACK], F32)
        x_loads = [(0, 1), (1, 2), (2, 4), (4, 8)]
        xraw = [sbuf("xraw%d" % i, [P, hi - lo, D_IN], U8) for i, (lo, hi) in enumerate(x_loads)]
        xraw_tile = [xraw[i][:, j - lo, :] for i, (lo, hi) in enumerate(x_loads) for j in range(lo, hi)]
        xwide = [sbuf("xwide%d" % j, [P, D_IN], BF16) for j in range(TILES)]
        xinter = [sbuf("xinter%d" % i, [P, D_IN], BF16) for i in range(4)]
        xcodes = [sbuf("xcodes%d" % j, [P, PASSES * P], U32) for j in range(TILES)]
        xscales = [sbuf("xscales%d" % j, [P, PASSES * P], U8) for j in range(TILES)]
        wwords = [sbuf("wwords%d" % c, [P, PASSES, 2 * CH], U8) for c in range(n_chunks)]
        wscales = [sbuf("wscales%d" % m, [P, PASSES, N_FEAT], U8) for m in range(2)]
        feat_group = [
            [sbuf("feat%d_%d" % (c, g), [P, PACK, CH], F32) for g in range(PASSES)] for c in range(n_chunks)
        ]
        feat = [[feat_group[c][j // PACK][:, j % PACK, :] for j in range(TILES)] for c in range(n_chunks)]
        squares = [sbuf("squares%d" % i, [P, CH], F32) for i in range(2 * TILES)]
        cast_group = sbuf("cast_group", [P, PACK, CH], BF16)
        inter = [sbuf("inter%d" % i, [P, PACK * CH], BF16) for i in range(4)]
        codes = [[sbuf("codes%d_%d" % (c, g), [P, CH], U32) for g in range(PASSES)] for c in range(n_chunks)]
        cscales = [[sbuf("cscales%d_%d" % (c, g), [P, CH], U8) for g in range(PASSES)] for c in range(n_chunks)]
        t_sb = sbuf("t_sb", [P, TILES], F32)
        root_t = sbuf("root_t", [P, TILES], F32)
        inv_root_t = sbuf("inv_root_t", [P, TILES], F32)
        inv_other = [sbuf("inv_q", [P, TILES], F32), sbuf("inv_p", [P, TILES], F32)]
        t_row = sbuf("t_row", [P, 1], F32)
        n_sb = sbuf("n_sb", [P, 1], F32)
        inv_n = sbuf("inv_n", [P, 1], F32)
        neg_t_over_n = sbuf("neg_t_over_n", [P, TILES], F32)
        th_sum = [sbuf("th_sum%d" % c, [P, BLOCKS], F32) for c in range(n_chunks)]
        var = [sbuf("var%d" % c, [P, BLOCKS], F32) for c in range(n_chunks)]
        std = [sbuf("std%d" % c, [P, BLOCKS], F32) for c in range(n_chunks)]
        inv_std = [sbuf("inv_std%d" % c, [P, BLOCKS], F32) for c in range(n_chunks)]
        inv_std_rows = [sbuf("inv_std_rows%d" % h, [P, CH], F32) for h in range(2)]

        nc.scalar.dma_start(out=p_sb[:], in_=p.rearrange("(g m s) -> m g s", g=PASSES, s=PACK))
        nc.scalar.dma_start(out=q_sb[:], in_=q.rearrange("(g m s) -> m g s", g=PASSES, s=PACK))
        nc.scalar.dma_start(out=xs_sb[:], in_=x_scale.rearrange("o (g m s) -> m (o g) s", g=PASSES, s=PACK))
        for m in (MODEL_B, MODEL_A):
            nc.vector.memset(wscales[m][:].rearrange("p g n -> p (g n)").bitcast(I32), 0)
        make_identity(nc, ident[:])

        x_rows = x_bytes.rearrange("(g m s) k -> g m s k", g=PASSES, s=PACK)

        def load_x(i):
            lo, hi = x_loads[i]
            g = lo // PACK
            nc.sync.dma_start(out=xraw[i][:], in_=x_rows[g][:, lo - PACK * g : hi - PACK * g, :])

        def load_words(c):
            m, h = CHUNKS[c]
            words = [wa_words, wb_words][m].rearrange("g p n -> p g n")
            nc.sync.dma_start(
                out=wwords[c][:].bitcast(I32), in_=words[:, :, 2 * CH * h : 2 * CH * (h + 1)].bitcast(I32)
            )

        def load_scales(m):
            rows = [wa_scales, wb_scales][m].rearrange("g r n -> r g n")
            for quad in range(4):
                nc.sync.dma_start(
                    out=wscales[m][32 * quad : 32 * quad + 4, :, :].bitcast(I32),
                    in_=rows[4 * quad : 4 * quad + 4, :, :].bitcast(I32),
                )

        for i in range(3):
            load_x(i)
        load_scales(MODEL_B)
        load_words(0)
        load_x(3)
        load_scales(MODEL_A)
        for c in range(1, n_chunks):
            load_words(c)

        p_flat = p_sb[:].rearrange("p g s -> p (g s)")
        q_flat = q_sb[:].rearrange("p g s -> p (g s)")

        def token_weights():
            nc.vector.tensor_tensor(out=t_sb[:], in0=p_flat, in1=q_flat, op=ALU.mult)

        def root_of_weights():
            nc.scalar.activation(out=root_t[:], in_=t_sb[:], func=ACT.Sqrt)

        def weight_inverses():
            nc.vector.tensor_reduce(out=t_row[:], in_=t_sb[:], axis=AX.X, op=ALU.add)
            nc.vector.reciprocal(out=inv_other[MODEL_A][:], in_=q_flat)
            nc.vector.reciprocal(out=inv_other[MODEL_B][:], in_=p_flat)
            nc.vector.reciprocal(out=inv_root_t[:], in_=root_t[:])

        def spread(bank, columns):
            for f in range(columns.shape[1]):
                nc.tensor.transpose(
                    bank[:, f * P : (f + 1) * P], columns[:, f : f + 1].to_broadcast([P, P]), ident[:]
                )

        def sum_n():
            nc.vector.tensor_reduce(out=n_sb[:], in_=sum_bank[:, 0:P], axis=AX.X, op=ALU.add)

        def invert_n():
            nc.vector.reciprocal(out=inv_n[:], in_=n_sb[:])

        def centring_factor():
            nc.vector.tensor_scalar(
                out=neg_t_over_n[:], in0=t_sb[:], scalar1=inv_n[:, 0:1], scalar2=-1.0, op0=ALU.mult, op1=ALU.mult
            )

        def widen_x(j):
            if j < WIDEN_ON_VECTOR:
                nc.vector.tensor_copy(out=xwide[j][:], in_=xraw_tile[j].bitcast(FP8))
            else:
                nc.scalar.copy(out=xwide[j][:], in_=xraw_tile[j].bitcast(FP8))

        def turn_x(j):
            words = xwide[j][:].bitcast(F32)
            bank = banks[X_BANKS[j % 3]]
            for g in range(PASSES):
                for u in range(2):
                    col = (2 * g + u) * P
                    nc.tensor.transpose(bank[:, col : col + P], words[:, 256 * g + u : 256 * (g + 1) : 2], ident[:])

        def scale_x(j, g):
            src = banks[X_BANKS[j % 3]][:].bitcast(BF16).rearrange("p (g u r e) -> p g r u e", g=PASSES, u=2, e=2)
            dst = xinter[j % 4][:].rearrange("p (g r u e) -> p g r u e", g=PASSES, u=2, e=2)
            factor = xs_sb[:, g, :].rearrange("p (u e) -> p u e", u=2).unsqueeze(1).to_broadcast([P, P, 2, 2])
            nc.vector.tensor_tensor(out=dst[:, g, :, :, :], in0=src[:, g, :, :, :], in1=factor, op=ALU.mult)

        def quantise_x(j):
            nc.vector.quantize_mx(out=xcodes[j][:].bitcast(FP8X4), scales=xscales[j][:], in_=xinter[j % 4][:])

        def first_product(c, j):
            m, h = CHUNKS[c]
            for g in range(PASSES):
                nc.tensor.matmul_mx(
                    out=banks[H_BANKS[j % 4]][:],
                    lhsT=xcodes[j][:, g * P : (g + 1) * P].bitcast(FP8X4),
                    lhsT_scale=xscales[j][:, g * P : (g + 1) * P],
                    rhs=wwords[c][:, g, :].bitcast(FP4X4),
                    rhs_scale=wscales[m][:, g, h * CH : (h + 1) * CH],
                    start=(g == 0),
                    stop=(g == PASSES - 1),
                )

        def weighted_relu(c, j):
            bank = banks[H_BANKS[j % 4]]
            if (c, j) in RELU_ON_VECTOR:
                nc.vector.tensor_scalar(
                    out=feat[c][j], in0=bank[:], scalar1=0.0, scalar2=t_sb[:, j : j + 1], op0=ALU.max, op1=ALU.mult
                )
            else:
                nc.scalar.activation(out=feat[c][j], in_=bank[:], func=ACT.Relu, scale=t_sb[:, j : j + 1])

        def add_turned(bank, src, first, last):
            for f in range(BLOCKS):
                nc.tensor.matmul(
                    out=bank[:, f * P : (f + 1) * P],
                    lhsT=src[:, f * P : (f + 1) * P],
                    rhs=ident[:],
                    is_transpose=True,
                    start=(first and f == 0),
                    stop=(last and f == BLOCKS - 1),
                )

        def sum_tokens(dst, bank):
            nc.vector.tensor_reduce(
                out=dst[:], in_=bank[:].rearrange("p (f m) -> p f m", f=BLOCKS), axis=AX.X, op=ALU.add
            )

        def centre(c, j):
            nc.vector.scalar_tensor_tensor(
                out=feat[c][j], in0=banks[MEAN_BANKS[c % 2]][:], scalar=neg_t_over_n[:, j : j + 1], in1=feat[c][j],
                op0=ALU.mult, op1=ALU.add,
            )

        def square(c, j):
            nc.scalar.activation(
                out=squares[(c % 2) * TILES + j][:], in_=feat[c][j], func=ACT.Square, scale=inv_root_t[:, j : j + 1]
            )

        def cast(c, j):
            factor = inv_other[CHUNKS[c][0]][:, j : j + 1]
            if c == CAST_ON_VECTOR:
                nc.vector.tensor_scalar(
                    out=cast_group[:, j % PACK, :], in0=feat[c][j], scalar1=factor, scalar2=None, op0=ALU.mult
                )
            else:
                nc.scalar.activation(out=cast_group[:, j % PACK, :], in_=feat[c][j], func=ACT.Copy, scale=factor)

        def add_pair(c, j):
            even, odd = squares[(c % 2) * TILES + j], squares[(c % 2) * TILES + j + 1]
            nc.vector.tensor_tensor(out=even[:], in0=even[:], in1=odd[:], op=ALU.add)

        def interleave(c, g):
            dst = inter[INTER_BUFFER[c][g]][:].rearrange("p (a i s) -> p a s i", i=4, s=PACK)
            src = cast_group[:].rearrange("p s (a i) -> p a s i", i=4)
            if (c, g) == SCALAR_GROUP:
                nc.scalar.copy(out=dst, in_=src)
            else:
                nc.vector.tensor_copy(out=dst, in_=src)

        def scale_and_interleave(c, g):
            factor = inv_other[CHUNKS[c][0]][:, PACK * g : PACK * (g + 1)].unsqueeze(1).to_broadcast([P, CH, PACK])
            nc.gpsimd.tensor_tensor(
                out=inter[INTER_BUFFER[c][g]][:].rearrange("p (f s) -> p f s", s=PACK),
                in0=feat_group[c][g][:].rearrange("p s f -> p f s"),
                in1=factor,
                op=ALU.mult,
            )

        def quantise(c, g):
            nc.vector.quantize_mx(
                out=codes[c][g][:].bitcast(FP8X4), scales=cscales[c][g][:], in_=inter[INTER_BUFFER[c][g]][:]
            )

        def root_of_var(c):
            scale = 1.0 / 1024.0 if CHUNKS[c][0] == MODEL_A else 1.0
            nc.scalar.activation(out=std[c][:], in_=var[c][:], func=ACT.Sqrt, scale=scale)

        def invert_std(c):
            nc.vector.reciprocal(out=inv_std[c][:], in_=std[c][:])

        def copy_inv_std_rows(c):
            nc.scalar.copy(out=inv_std_rows[CHUNKS[c][1]][:], in_=sum_bank[:])

        def second_product(k):
            ca, f, cb = OUT_TILES[k]
            for g in range(PASSES):
                nc.tensor.matmul_mx(
                    out=banks[OUT_BANKS[k]][:],
                    lhsT=codes[ca][g][:, f * P : (f + 1) * P].bitcast(FP8X4),
                    lhsT_scale=cscales[ca][g][:, f * P : (f + 1) * P],
                    rhs=codes[cb][g][:].bitcast(FP8X4),
                    rhs_scale=cscales[cb][g][:],
                    start=(g == 0),
                    stop=(g == PASSES - 1),
                )

        def finish(k):
            ca, f, cb = OUT_TILES[k]
            stage = feat[k // TILES][k % TILES]
            nc.vector.scalar_tensor_tensor(
                out=stage, in0=banks[OUT_BANKS[k]][:], scalar=inv_std[ca][:, f : f + 1],
                in1=inv_std_rows[CHUNKS[cb][1]][:], op0=ALU.mult, op1=ALU.mult,
            )
            row = CHUNKS[ca][1] * CH + f * P
            col = CHUNKS[cb][1] * CH
            nc.sync.dma_start(out=out[row : row + P, col : col + CH], in_=stage)

        steps = {}
        last_writer = {}
        readers = {}

        def step(key, call, reads, writes):
            after = set(last_writer[r] for r in reads + writes if r in last_writer)
            for w in writes:
                after = after | set(readers.get(w, []))
                readers[w] = []
                last_writer[w] = key
            for r in reads:
                readers.setdefault(r, []).append(key)
            steps[key] = (call, after)

        step(("t",), token_weights, [], ["t"])
        step(("root_t",), root_of_weights, ["t"], ["root_t"])
        step(("inverses",), weight_inverses, ["root_t"], ["inverses"])
        step(("spread_t",), partial(spread, sum_bank, t_row[:]), ["inverses"], [("bank", SUM_BANK)])
        step(("n", 0), sum_n, [("bank", SUM_BANK)], ["n"])
        step(("n", 1), invert_n, ["n"], ["inv_n"])
        step(("n", 2), centring_factor, ["inv_n"], ["t_over_n"])
        for j in range(TILES):
            x_bank = ("bank", X_BANKS[j % 3])
            step(("widen", j), partial(widen_x, j), [], [("xwide", j)])
            step(("turn", j), partial(turn_x, j), [("xwide", j)], [x_bank])
            for g in range(PASSES):
                step(("scale", j, g), partial(scale_x, j, g), [x_bank], [("xinter", j % 4, g)])
            step(("xquant", j), partial(quantise_x, j), [("xinter", j % 4, g) for g in range(PASSES)], [("xcodes", j)])
        for c in range(n_chunks):
            for j in range(TILES):
                h_bank = ("bank", H_BANKS[j % 4])
                step(("mx1", c, j), partial(first_product, c, j), [("xcodes", j)], [h_bank])
                step(("relu", c, j), partial(weighted_relu, c, j), [h_bank, "t"], [("feat", c, j)])
                step(("add_th", c, j), partial(add_turned, sum_bank, feat[c][j], j == 0, j == TILES - 1),
                     [("feat", c, j)], [("bank", SUM_BANK)])
            step(("sum_th", c), partial(sum_tokens, th_sum[c], sum_bank), [("bank", SUM_BANK)], [("th_sum", c)])
        for c in range(n_chunks):
            mean_bank = ("bank", MEAN_BANKS[c % 2])
            var_bank = ("bank", VAR_BANKS[c])
            step(("spread_th", c), partial(spread, banks[MEAN_BANKS[c % 2]], th_sum[c][:]), [("th_sum", c)],
                 [mean_bank])
            for j in range(TILES):
                step(("centre", c, j), partial(centre, c, j), [mean_bank, "t_over_n"], [("feat", c, j)])
                step(("square", c, j), partial(square, c, j), [("feat", c, j)], [("squares", c % 2, j)])
            added = range(0, TILES, 2) if c in PAIRED_CHUNKS else range(TILES)
            for j in added:
                if c in PAIRED_CHUNKS:
                    step(("pair", c, j), partial(add_pair, c, j), [("squares", c % 2, j + 1)], [("squares", c % 2, j)])
                src = squares[(c % 2) * TILES + j][:]
                step(("add_sq", c, j), partial(add_turned, banks[VAR_BANKS[c]], src, j == added[0], j == added[-1]),
                     [("squares", c % 2, j)], [var_bank])
            for g in range(PASSES):
                tiles = range(PACK * g, PACK * (g + 1))
                buffer = ("inter", INTER_BUFFER[c][g])
                if (c, g) in POOL_GROUPS:
                    step(("pool", c, g), partial(scale_and_interleave, c, g), [("feat", c, j) for j in tiles], [buffer])
                else:
                    for j in tiles:
                        step(("cast", c, j), partial(cast, c, j), [("feat", c, j)], [("cast", j % PACK)])
                    step(("inter", c, g), partial(interleave, c, g), [("cast", s) for s in range(PACK)], [buffer])
                step(("quant", c, g), partial(quantise, c, g), [buffer], [("codes", c, g)])
            step(("sum_sq", c), partial(sum_tokens, var[c], banks[VAR_BANKS[c]]), [var_bank], [("var", c)])
            step(("root", c), partial(root_of_var, c), [("var", c)], [("std", c)])
            step(("invert", c), partial(invert_std, c), [("std", c)], [("inv_std", c)])
        for c in range(n_chunks):
            if CHUNKS[c][0] == MODEL_B:
                step(("spread_std", c), partial(spread, sum_bank, inv_std[c][:]), [("inv_std", c)],
                     [("bank", SUM_BANK)])
                step(("rows", c), partial(copy_inv_std_rows, c), [("bank", SUM_BANK)], [("rows", c)])
        for k, (ca, f, cb) in enumerate(OUT_TILES):
            out_bank = ("bank", OUT_BANKS[k])
            step(("mx2", k), partial(second_product, k), [("codes", c, g) for c in (ca, cb) for g in range(PASSES)],
                 [out_bank])
            step(("finish", k), partial(finish, k), [out_bank, ("inv_std", ca), ("rows", cb)],
                 [("feat",) + divmod(k, TILES)])

        def run(name, c, lo=0, hi=TILES):
            return [(name, c, j) for j in range(lo, hi)]

        def pairs(name, c):
            return [(name, c, j) for j in range(0, TILES, 2)]

        def each(name, lo, hi):
            return [(name, k) for k in range(lo, hi)]

        pe = each("turn", 0, 2) + [("spread_t",)] + each("turn", 2, 4)
        for j in range(4):
            pe = pe + [("mx1", 0, j), ("turn", j + 4)] + run("add_th", 0, max(j - 2, 0), max(j - 1, 0))
        pe = pe + run("mx1", 0, 4, 6) + run("add_th", 0, 2, 4) + run("mx1", 0, 6, 7) + run("add_th", 0, 4, 6)
        pe = pe + run("mx1", 0, 7) + run("mx1", 1, 0, 1) + run("add_th", 0, 6) + run("mx1", 1, 1, 3)
        pe = pe + [("spread_th", 0)] + run("mx1", 1, 3)
        pe = pe + run("add_th", 1) + run("mx1", 2, 0, 2) + [("spread_th", 1)] + run("mx1", 2, 2)
        pe = pe + run("add_th", 2) + pairs("add_sq", 0) + [("spread_th", 2)]
        pe = pe + run("mx1", 3) + run("add_th", 3) + run("add_sq", 1, 0, 4) + [("spread_th", 3)]
        pe = pe + run("add_sq", 1, 4) + [("spread_std", 0)] + run("add_sq", 2) + each("mx2", 0, 4)
        pe = pe + run("add_sq", 3, 0, 4) + [("spread_std", 2)] + each("mx2", 4, 6) + run("add_sq", 3, 4)
        pe = pe + each("mx2", 6, len(OUT_TILES))

        act = [("root_t",)] + each("widen", WIDEN_ON_VECTOR, 7) + run("relu", 0, 0, 1) + [("widen", 7)]
        act = act + run("relu", 0, 1) + [key for key in run("relu", 1) if key[1:] not in RELU_ON_VECTOR]
        act = act + run("square", 0) + run("relu", 2) + run("cast", 1, 0, PACK) + run("square", 1, 0, 4)
        act = act + run("relu", 3) + run("square", 1, 4)
        act = act + [("root", 0)] + run("square", 2) + [("rows", 0)]
        act = act + run("cast", 3, 0, PACK) + run("square", 3, 0, 2) + [("root", 1)] + run("square", 3, 2, 4)
        act = act + [("root", 2)] + run("square", 3, 4, 7) + [("rows", 2)] + run("square", 3, 7)
        act = act + [("inter", 3, 0), ("root", 3)]

        dve = [("widen", 0), ("t",), ("widen", 1), ("inverses",), ("scale", 0, 0), ("scale", 0, 1)]
        for j in range(1, TILES):
            dve = dve + [("scale", j, 0), ("xquant", j - 1), ("scale", j, 1)] + each("n", j - 1, min(j, 3))
        dve = dve + [("xquant", TILES - 1), ("sum_th", 0)]
        dve = dve + run("centre", 0, 0, 4) + [("relu",) + key for key in RELU_ON_VECTOR] + run("centre", 0, 4)
        dve = dve + [("sum_th", 1)] + run("centre", 1)
        dve = dve + pairs("pair", 0) + [("sum_th", 2), ("inter", 1, 0), ("quant", 0, 0), ("quant", 0, 1)]
        dve = dve + run("centre", 2, 0, 4) + [("sum_sq", 0)] + run("centre", 2, 4)
        dve = dve + run("cast", 2, 0, PACK) + [("quant", 1, 0), ("sum_th", 3), ("inter", 2, 0), ("invert", 0)]
        dve = dve + [("quant", 1, 1), ("quant", 2, 0)]
        dve = dve + run("centre", 3) + [("sum_sq", 1), ("quant", 2, 1), ("sum_sq", 2), ("invert", 1)]
        dve = dve + [("finish", 0), ("invert", 2)] + each("finish", 1, 6) + [("quant", 3, 1), ("sum_sq", 3)]
        dve = dve + [("quant", 3, 0), ("invert", 3)] + each("finish", 6, len(OUT_TILES))

        pool = [("pool", c, g) for c, g in POOL_GROUPS]

        queues = [pe, act, dve, pool]
        assert sorted(pe + act + dve + pool) == sorted(steps)
        done = set()
        heads = [0] * len(queues)
        while len(done) < len(steps):
            moved = False
            for e, queue in enumerate(queues):
                if heads[e] < len(queue) and steps[queue[heads[e]]][1] <= done:
                    steps[queue[heads[e]]][0]()
                    done.add(queue[heads[e]])
                    heads[e] = heads[e] + 1
                    moved = True
            assert moved
